import numpy as np
import ml_dtypes


def mxq(x, axis, fmt="e4m3"):
    dtype, down = {"e4m3": (ml_dtypes.float8_e4m3fn, 7), "e5m2": (ml_dtypes.float8_e5m2, 14)}[fmt]
    v = np.moveaxis(np.asarray(x, np.float32).astype(ml_dtypes.bfloat16).astype(np.float64), axis, -1)
    blocks = v.reshape(v.shape[:-1] + (-1, 32))
    amax = np.abs(blocks).max(-1, keepdims=True)
    byte = np.maximum(np.where(amax > 0, np.frexp(amax)[1] - 1 + 127, 0) - down, 1)
    scale = np.exp2(byte - 127.0)
    codes = (blocks / scale).astype(np.float32).astype(dtype).astype(np.float64)
    return np.moveaxis((codes * scale).reshape(v.shape), -1, axis)


WIDE = False


def mx_kscale(k):
    if not WIDE:
        return np.ones(k)
    levels = np.array([10, -10, 5, -5, 0])
    if k % 512:
        return np.exp2(np.random.permutation(np.resize(levels, k // 32))).repeat(32)
    a = np.empty((k // 512, 16))
    for p in range(k // 512):
        a[p, :8] = np.random.permutation(np.resize(levels, 8))
        for g in range(8):
            far = levels[np.abs(levels - a[p, g]) >= 10]
            a[p, g + 8] = far[np.random.randint(len(far))]
    return np.exp2(a.ravel()).repeat(32)


def f64(x):
    return np.asarray(x).astype(np.float64)


def striped(idx):
    return np.tile(idx.reshape(-1, 16).T, (8, 1)).astype(np.uint16)


def unstriped(offs):
    return offs[:16].T.reshape(-1).astype(np.int64)


def striped8(idx):
    return np.concatenate([v.reshape(-1, 16).T for v in idx]).astype(np.uint16)


def unstriped8(offs):
    return np.stack([offs[16 * g:16 * g + 16].T.reshape(-1) for g in range(8)]).astype(np.int64)


E2M1 = np.array([0.0, 0.5, 1.0, 1.5, 2.0, 3.0, 4.0, 6.0, -0.0, -0.5, -1.0, -1.5, -2.0, -3.0, -4.0, -6.0])


def pack_weight(w, fmt):
    k, n = w.shape
    w = f64(np.asarray(w, np.float32).astype(ml_dtypes.bfloat16)).reshape(k // 32, 32, n)
    amax = np.abs(w).max(1)
    if fmt == "e4m3":
        byte = np.frexp(amax)[1] - 1 + 127 - 7
    else:
        mant, ex = np.frexp(amax / 6.0)
        byte = np.where(mant > 0.5, ex, ex - 1) + 127
    byte = np.clip(np.where(amax > 0, byte, 1), 1, 254)
    scaled = (w * np.exp2(127.0 - byte)[:, None, :]).reshape(k, n).astype(np.float32)
    by_word = np.ascontiguousarray(scaled.reshape(k // 512, 128, 4, n).transpose(0, 1, 3, 2))
    if fmt == "e4m3":
        words = by_word.astype(ml_dtypes.float8_e4m3fn).view(np.uint8)
    else:
        c = by_word.astype(ml_dtypes.float4_e2m1fn).view(np.uint8) & 0xF
        words = (c[..., 0::2] | (c[..., 1::2] << 4)).reshape(k // 512, 128, 2 * n)
    return np.ascontiguousarray(words), np.ascontiguousarray(byte.astype(np.uint8).reshape(k // 512, 16, n))


def unpack_weight(words, scales, fmt):
    g, _, n = scales.shape
    words = np.ascontiguousarray(words).reshape(g, 128, n, -1)
    if fmt == "e4m3":
        vals = words.view(ml_dtypes.float8_e4m3fn).astype(np.float64)
    else:
        nib = np.empty((g, 128, n, 4), np.uint8)
        nib[..., 0::2] = words & 0xF
        nib[..., 1::2] = words >> 4
        vals = E2M1[nib]
    vals = vals * np.repeat(np.exp2(scales.astype(np.float64) - 127.0), 8, axis=1)[..., None]
    return vals.transpose(0, 1, 3, 2).reshape(g * 512, n)


def pack_table(v):
    words, scales = pack_weight(v, "e4m3")
    return np.concatenate([words.reshape(words.shape[0], -1), scales.reshape(scales.shape[0], -1)], axis=1)


def unpack_table(tab):
    g, t = tab.shape[0], tab.shape[1] // 528
    return unpack_weight(tab[:, :512 * t].reshape(g, 128, t, 4), tab[:, 512 * t:].reshape(g, 16, t), "e4m3")


def silu(v):
    return v / (1.0 + np.exp(-np.maximum(v, -700.0)))


K, M, T, S = 512, 256, 2048, 1024


def setup_inputs():
    n = np.random.standard_normal
    s = mx_kscale(K)[:, None]
    p_w4 = pack_weight(n((K, M)) / np.sqrt(K) / s, "e2m1")
    return {
        "tab": pack_table(n((K, T)) * s),
        "w4_words": p_w4[0],
        "w4_scales": p_w4[1],
        "w8": (n((K, M)) / np.sqrt(K) / s).astype(np.float32),
        "wgo": np.repeat(np.random.uniform(0.5, 2.0, (8, S)), 16, axis=0).astype(np.float32),
        "offs": striped(np.random.permutation(T)[:S]),
        "offs2": striped8(np.stack([np.random.permutation(T)[:S] for _ in range(8)])),
    }


def reference(tab, w4_words, w4_scales, w8, wgo, offs, offs2):
    tab_ = unpack_table(tab)[:, unstriped(offs)]
    w4_ = unpack_weight(w4_words, w4_scales, "e2m1")
    w8_ = mxq(f64(w8), 0, "e4m3")
    y = w4_.T @ tab_
    u = w8_.T @ tab_
    y = silu(y) * u
    place = unstriped8(offs2)[np.arange(M) % 128 // 16]
    out = np.zeros((M, T))
    out[np.arange(M)[:, None], place] = f64(wgo)[np.arange(M) % 128] * (y)
    return out

@@ -1,0 +1,119 @@
+from contextlib import ExitStack
+
+import concourse.mybir as mybir
+
+K, M, T, S = 512, 256, 2048, 1024
+FLOPS = 2 * 2 * K * M * S
+
+F32 = mybir.dt.float32
+BF16 = mybir.dt.bfloat16
+I32 = mybir.dt.int32
+U32 = mybir.dt.uint32
+U16 = mybir.dt.uint16
+U8 = mybir.dt.uint8
+FP8X4 = mybir.dt.float8_e4m3fn_x4
+FP4X4 = mybir.dt.float4_e2m1fn_x4
+MULT = mybir.AluOpType.mult
+SILU = mybir.ActivationFunctionType.Silu
+
+P = 128
+PACK = 4
+HALF = 512
+STRIPE = 16
+HOLD = 8
+
+
+def load_scale_rows(nc, plane, rows):
+    for q in range(4):
+        nc.sync.dma_start(out=plane[32 * q : 32 * q + 4, :], in_=rows[4 * q : 4 * q + 4, :])
+
+
+def tile_list_tabhs_g_none_kernel(tc, tab, w4_words, w4_scales, w8, wgo, offs, offs2, out):
+    nc = tc.nc
+    with ExitStack() as ctx:
+        keep = ctx.enter_context(tc.tile_pool(name="keep", bufs=1))
+        psum = ctx.enter_context(tc.psum_pool(name="psum", bufs=1))
+
+        pick = keep.tile([P, S // STRIPE], U16, name="pick")
+        nc.sync.dma_start(pick[:], offs)
+
+        w8_raw = keep.tile([P, PACK, M], F32, name="w8_raw")
+        nc.sync.dma_start(out=w8_raw[:], in_=w8.rearrange("(p i) n -> p i n", i=PACK))
+
+        tab_scales = keep.tile([P, T // 4], I32, name="tab_scales", align_bytes=64)
+        nc.vector.memset(tab_scales[:], 0)
+        load_scale_rows(nc, tab_scales, tab[0, K * T :].bitcast(I32).rearrange("(q t) -> q t", q=16))
+
+        tab_words = keep.tile([P, T], I32, name="tab_words", tag="shared", align_bytes=64)
+        nc.vector.memset(tab_words[:, :HOLD], 0)
+        nc.sync.dma_start(out=tab_words[:], in_=tab[0, : K * T].bitcast(I32).rearrange("(p t) -> p t", p=P))
+
+        w4 = keep.tile([P, M // 4 + M // 2], I32, name="w4", align_bytes=64)
+        w4_plane, w4_codes = w4[:, : M // 4], w4[:, M // 4 :]
+        nc.vector.memset(w4[:, : M // 4 + HOLD], 0)
+        nc.sync.dma_start(out=w4_codes, in_=w4_words[0].bitcast(I32))
+        load_scale_rows(nc, w4_plane, w4_scales[0].bitcast(I32))
+
+        weights = keep.tile([P, S], F32, name="weights")
+        nc.vector.memset(weights[:, HALF - HOLD : HALF + HOLD], 0.0)
+        for h in range(2):
+            nc.sync.dma_start(out=weights[:, h * HALF : (h + 1) * HALF], in_=wgo[:, h * HALF : (h + 1) * HALF])
+        place = keep.tile([P, S // STRIPE], U16, name="place")
+        nc.sync.dma_start(place[:], offs2)
+
+        warm = keep.tile([P, 8], F32, name="warm")
+        nc.gpsimd.memset(warm[:, 0:1], 0.0)
+        nc.scalar.activation(warm[:, 4:5], warm[:, 0:1], SILU)
+
+        window0 = keep.tile([P, T], F32, name="window0")
+        nc.vector.memset(window0[:], 0.0)
+
+        cols = HALF // STRIPE
+        got_scales = [keep.tile([P, HALF], U8, name="got_scales%d" % h, align_bytes=64) for h in range(2)]
+        got_words = [keep.tile([P, HALF], U32, name="got_words%d" % h, align_bytes=64) for h in range(2)]
+        for h in range(2):
+            nc.vector.tensor_copy(got_scales[h][:], tab_scales[:].bitcast(U8).indirect(pick[:, h * cols : (h + 1) * cols]))
+
+        w8_bf = keep.tile([P, M, PACK], BF16, name="w8_bf", align_bytes=64)
+        nc.scalar.copy(w8_bf[:], w8_raw[:].rearrange("p i n -> p n i"))
+        w8_codes = keep.tile([P, M], U32, name="w8_codes", align_bytes=64)
+        w8_plane = keep.tile([P, M], U8, name="w8_plane", align_bytes=64)
+        nc.vector.quantize_mx(out=w8_codes[:].bitcast(FP8X4), scales=w8_plane[:], in_=w8_bf[:].rearrange("p n i -> p (n i)"))
+
+        for h in range(2):
+            nc.vector.tensor_copy(got_words[h][:], tab_words[:].bitcast(U32).indirect(pick[:, h * cols : (h + 1) * cols]))
+
+        window1 = keep.tile([P, T], F32, name="window1", tag="shared", align_bytes=64)
+        nc.gpsimd.memset(window1[:], 0.0)
+        windows = [window0, window1]
+
+        for m in range(2):
+            for h in range(2):
+                gate = psum.tile([P, HALF], F32, name="gate%d%d" % (m, h))
+                up = psum.tile([P, HALF], F32, name="up%d%d" % (m, h))
+                nc.tensor.matmul_mx(
+                    out=gate[:],
+                    lhsT=w4_codes.bitcast(U8)[:, 2 * P * m : 2 * P * (m + 1)].bitcast(FP4X4),
+                    lhsT_scale=w4_plane.bitcast(U8)[:, P * m : P * (m + 1)],
+                    rhs=got_words[h][:].bitcast(FP8X4),
+                    rhs_scale=got_scales[h][:],
+                    start=True,
+                    stop=True,
+                )
+                nc.tensor.matmul_mx(
+                    out=up[:],
+                    lhsT=w8_codes[:, P * m : P * (m + 1)].bitcast(FP8X4),
+                    lhsT_scale=w8_plane[:, P * m : P * (m + 1)],
+                    rhs=got_words[h][:].bitcast(FP8X4),
+                    rhs_scale=got_scales[h][:],
+                    start=True,
+                    stop=True,
+                )
+                gated = keep.tile([P, HALF], F32, name="gated%d%d" % (m, h))
+                nc.scalar.activation(gated[:], gate[:], SILU)
+                weighted = keep.tile([P, HALF], F32, name="weighted%d%d" % (m, h))
+                nc.vector.tensor_tensor(weighted[:], up[:], weights[:, h * HALF : (h + 1) * HALF], MULT)
+                nc.vector.tensor_tensor(
+                    windows[m][:].indirect(place[:, h * cols : (h + 1) * cols]), gated[:], weighted[:], MULT
+                )
+            nc.sync.dma_start(out=out[P * m : P * (m + 1), :], in_=windows[m][:])

@@ -1,6 +1,7 @@
 from contextlib import ExitStack
 
 import concourse.mybir as mybir
+from concourse.masks import make_identity
 
 K, M, T, S = 512, 256, 2048, 1024
 FLOPS = 2 * 2 * K * M * S
@@ -15,12 +16,15 @@ FP8X4 = mybir.dt.float8_e4m3fn_x4
 FP4X4 = mybir.dt.float4_e2m1fn_x4
 MULT = mybir.AluOpType.mult
 SILU = mybir.ActivationFunctionType.Silu
+COPY = mybir.ActivationFunctionType.Copy
 
 P = 128
 PACK = 4
 HALF = 512
 STRIPE = 16
+GROUPS = 8
 HOLD = 8
+EARLY = 512
 
 
 def load_scale_rows(nc, plane, rows):
@@ -36,17 +40,19 @@ def tile_list_tabhs_g_none_kernel(tc, tab, w4_words, w4_scales, w8, wgo, offs, o
 
         pick = keep.tile([P, S // STRIPE], U16, name="pick")
         nc.sync.dma_start(pick[:], offs)
-
-        w8_raw = keep.tile([P, PACK, M], F32, name="w8_raw")
-        nc.sync.dma_start(out=w8_raw[:], in_=w8.rearrange("(p i) n -> p i n", i=PACK))
+        tab_words = keep.tile([P, T], I32, name="tab_words", tag="shared", align_bytes=64)
+        words_hbm = tab[0, : K * T].bitcast(I32).rearrange("(p t) -> p t", p=P)
+        nc.sync.dma_start(out=tab_words[:, :EARLY], in_=words_hbm[:, :EARLY])
 
         tab_scales = keep.tile([P, T // 4], I32, name="tab_scales", align_bytes=64)
         nc.vector.memset(tab_scales[:], 0)
         load_scale_rows(nc, tab_scales, tab[0, K * T :].bitcast(I32).rearrange("(q t) -> q t", q=16))
 
-        tab_words = keep.tile([P, T], I32, name="tab_words", tag="shared", align_bytes=64)
-        nc.vector.memset(tab_words[:, :HOLD], 0)
-        nc.sync.dma_start(out=tab_words[:], in_=tab[0, : K * T].bitcast(I32).rearrange("(p t) -> p t", p=P))
+        w8_raw = keep.tile([P, PACK, M], F32, name="w8_raw")
+        nc.vector.memset(w8_raw[:, 0, :HOLD], 0.0)
+        nc.sync.dma_start(out=w8_raw[:], in_=w8.rearrange("(p i) n -> p i n", i=PACK))
+        nc.vector.memset(tab_words[:, EARLY : EARLY + HOLD], 0)
+        nc.sync.dma_start(out=tab_words[:, EARLY:], in_=words_hbm[:, EARLY:])
 
         w4 = keep.tile([P, M // 4 + M // 2], I32, name="w4", align_bytes=64)
         w4_plane, w4_codes = w4[:, : M // 4], w4[:, M // 4 :]
@@ -61,9 +67,12 @@ def tile_list_tabhs_g_none_kernel(tc, tab, w4_words, w4_scales, w8, wgo, offs, o
         place = keep.tile([P, S // STRIPE], U16, name="place")
         nc.sync.dma_start(place[:], offs2)
 
-        warm = keep.tile([P, 8], F32, name="warm")
-        nc.gpsimd.memset(warm[:, 0:1], 0.0)
-        nc.scalar.activation(warm[:, 4:5], warm[:, 0:1], SILU)
+        warm = keep.tile([P, 16], F32, name="warm")
+        nc.vector.memset(warm[:, :HOLD], 0.0)
+        nc.scalar.activation(warm[:, HOLD : HOLD + 1], warm[:, 0:1], SILU)
+        ident = keep.tile([P, P], F32, name="ident")
+        nc.vector.memset(ident[:, :HOLD], 0.0)
+        make_identity(nc, ident[:])
 
         window0 = keep.tile([P, T], F32, name="window0")
         nc.vector.memset(window0[:], 0.0)
@@ -87,33 +96,81 @@ def tile_list_tabhs_g_none_kernel(tc, tab, w4_words, w4_scales, w8, wgo, offs, o
         nc.gpsimd.memset(window1[:], 0.0)
         windows = [window0, window1]
 
+        def gate_pass(m, h):
+            gate = psum.tile([P, HALF], F32, name="gate%d%d" % (m, h), tag="gate%d%d" % (m, h))
+            nc.tensor.matmul_mx(
+                out=gate[:],
+                lhsT=w4_codes.bitcast(U8)[:, 2 * P * m : 2 * P * (m + 1)].bitcast(FP4X4),
+                lhsT_scale=w4_plane.bitcast(U8)[:, P * m : P * (m + 1)],
+                rhs=got_words[h][:].bitcast(FP8X4),
+                rhs_scale=got_scales[h][:],
+                start=True,
+                stop=True,
+            )
+            gated = keep.tile([P, HALF], F32, name="gated%d%d" % (m, h))
+            nc.scalar.activation(gated[:], gate[:], SILU)
+            return gated
+
+        def up_pass(m, h):
+            up = psum.tile([P, HALF], F32, name="up%d%d" % (m, h), tag="up%d%d" % (m, h))
+            nc.tensor.matmul_mx(
+                out=up[:],
+                lhsT=w8_codes[:, P * m : P * (m + 1)].bitcast(FP8X4),
+                lhsT_scale=w8_plane[:, P * m : P * (m + 1)],
+                rhs=got_words[h][:].bitcast(FP8X4),
+                rhs_scale=got_scales[h][:],
+                start=True,
+                stop=True,
+            )
+            weighted = keep.tile([P, HALF], F32, name="weighted%d%d" % (m, h))
+            nc.vector.tensor_tensor(weighted[:], up[:], weights[:, h * HALF : (h + 1) * HALF], MULT)
+            return weighted
+
+        def scatter(m, h, gated, weighted):
+            nc.vector.tensor_tensor(
+                windows[m][:].indirect(place[:, h * cols : (h + 1) * cols]), gated[:], weighted[:], MULT
+            )
+
+        first = [(up_pass(m, 0), gate_pass(m, 0)) for m in range(2)]
         for m in range(2):
-            for h in range(2):
-                gate = psum.tile([P, HALF], F32, name="gate%d%d" % (m, h))
-                up = psum.tile([P, HALF], F32, name="up%d%d" % (m, h))
+            scatter(m, 0, first[m][1], first[m][0])
+
+        tiles = HALF // P
+        turned = psum.tile([P, tiles, P], F32, name="turned", tag="gate00")
+        for c in range(tiles):
+            nc.tensor.transpose(turned[:, c, :], weights[:, HALF + P * c : HALF + P * (c + 1)], ident[:])
+        token_weights = keep.tile([P, tiles, GROUPS], F32, name="token_weights")
+        nc.scalar.copy(token_weights[:], turned[:].rearrange("p c (g s) -> p c g s", s=STRIPE)[:, :, :, 0])
+
+        scaled = keep.tile([P, tiles, M], F32, name="scaled")
+        for pair in range(tiles // 2):
+            up_t = psum.tile([P, 2, M], F32, name="up_t%d" % pair, tag="gate%d0" % (1 - pair))
+            for i in range(2):
+                c = 2 * pair + i
                 nc.tensor.matmul_mx(
-                    out=gate[:],
-                    lhsT=w4_codes.bitcast(U8)[:, 2 * P * m : 2 * P * (m + 1)].bitcast(FP4X4),
-                    lhsT_scale=w4_plane.bitcast(U8)[:, P * m : P * (m + 1)],
-                    rhs=got_words[h][:].bitcast(FP8X4),
-                    rhs_scale=got_scales[h][:],
+                    out=up_t[:, i, :],
+                    lhsT=got_words[1][:, P * c : P * (c + 1)].bitcast(FP8X4),
+                    lhsT_scale=got_scales[1][:, P * c : P * (c + 1)],
+                    rhs=w8_codes[:].bitcast(FP8X4),
+                    rhs_scale=w8_plane[:],
                     start=True,
                     stop=True,
                 )
-                nc.tensor.matmul_mx(
-                    out=up[:],
-                    lhsT=w8_codes[:, P * m : P * (m + 1)].bitcast(FP8X4),
-                    lhsT_scale=w8_plane[:, P * m : P * (m + 1)],
-                    rhs=got_words[h][:].bitcast(FP8X4),
-                    rhs_scale=got_scales[h][:],
-                    start=True,
-                    stop=True,
-                )
-                gated = keep.tile([P, HALF], F32, name="gated%d%d" % (m, h))
-                nc.scalar.activation(gated[:], gate[:], SILU)
-                weighted = keep.tile([P, HALF], F32, name="weighted%d%d" % (m, h))
-                nc.vector.tensor_tensor(weighted[:], up[:], weights[:, h * HALF : (h + 1) * HALF], MULT)
-                nc.vector.tensor_tensor(
-                    windows[m][:].indirect(place[:, h * cols : (h + 1) * cols]), gated[:], weighted[:], MULT
-                )
+            for i in range(2):
+                c = 2 * pair + i
+                for g in range(GROUPS):
+                    nc.scalar.activation(
+                        scaled[:, c, :].rearrange("p (m g s) -> p m g s", m=2, s=STRIPE)[:, :, g, :],
+                        up_t[:, i, :].rearrange("p (m g s) -> p m g s", m=2, s=STRIPE)[:, :, g, :],
+                        COPY,
+                        scale=token_weights[:, c, g : g + 1],
+                    )
+        for m in range(2):
+            back = psum.tile([P, tiles, P], F32, name="back%d" % m, tag="up%d0" % m)
+            for c in range(tiles):
+                nc.tensor.transpose(back[:, c, :], scaled[:, c, P * m : P * (m + 1)], ident[:])
+            weighted = keep.tile([P, HALF], F32, name="weighted%d1" % m)
+            gated = gate_pass(m, 1)
+            nc.scalar.copy(weighted[:], back[:].rearrange("p c j -> p (c j)"))
+            scatter(m, 1, gated, weighted)
             nc.sync.dma_start(out=out[P * m : P * (m + 1), :], in_=windows[m][:])

@@ -75,13 +75,13 @@ def tile_list_tabhs_g_none_kernel(tc, tab, w4_words, w4_scales, w8, wgo, offs, o
         make_identity(nc, ident[:])
 
         window0 = keep.tile([P, T], F32, name="window0")
-        nc.vector.memset(window0[:], 0.0)
+        nc.vector.memset(window0[:].bitcast(I32), 0)
 
         cols = HALF // STRIPE
-        got_scales = [keep.tile([P, HALF], U8, name="got_scales%d" % h, align_bytes=64) for h in range(2)]
+        all_scales = keep.tile([P, S], U8, name="all_scales", align_bytes=64)
+        got_scales = [all_scales[:, h * HALF : (h + 1) * HALF] for h in range(2)]
         got_words = [keep.tile([P, HALF], U32, name="got_words%d" % h, align_bytes=64) for h in range(2)]
-        for h in range(2):
-            nc.vector.tensor_copy(got_scales[h][:], tab_scales[:].bitcast(U8).indirect(pick[:, h * cols : (h + 1) * cols]))
+        nc.vector.tensor_copy(all_scales[:], tab_scales[:].bitcast(U8).indirect(pick[:]))
 
         w8_bf = keep.tile([P, M, PACK], BF16, name="w8_bf", align_bytes=64)
         nc.scalar.copy(w8_bf[:], w8_raw[:].rearrange("p i n -> p n i"))
@@ -89,8 +89,12 @@ def tile_list_tabhs_g_none_kernel(tc, tab, w4_words, w4_scales, w8, wgo, offs, o
         w8_plane = keep.tile([P, M], U8, name="w8_plane", align_bytes=64)
         nc.vector.quantize_mx(out=w8_codes[:].bitcast(FP8X4), scales=w8_plane[:], in_=w8_bf[:].rearrange("p n i -> p (n i)"))
 
-        for h in range(2):
-            nc.vector.tensor_copy(got_words[h][:], tab_words[:].bitcast(U32).indirect(pick[:, h * cols : (h + 1) * cols]))
+        part = HALF // 2
+        for lo, hi in ((0, part), (part, HALF), (HALF, S)):
+            nc.vector.tensor_copy(
+                got_words[lo // HALF][:, lo % HALF : lo % HALF + hi - lo],
+                tab_words[:].bitcast(U32).indirect(pick[:, lo // STRIPE : hi // STRIPE]),
+            )
 
         window1 = keep.tile([P, T], F32, name="window1", tag="shared", align_bytes=64)
         nc.gpsimd.memset(window1[:], 0.0)
@@ -103,7 +107,7 @@ def tile_list_tabhs_g_none_kernel(tc, tab, w4_words, w4_scales, w8, wgo, offs, o
                 lhsT=w4_codes.bitcast(U8)[:, 2 * P * m : 2 * P * (m + 1)].bitcast(FP4X4),
                 lhsT_scale=w4_plane.bitcast(U8)[:, P * m : P * (m + 1)],
                 rhs=got_words[h][:].bitcast(FP8X4),
-                rhs_scale=got_scales[h][:],
+                rhs_scale=got_scales[h],
                 start=True,
                 stop=True,
             )
@@ -113,15 +117,16 @@ def tile_list_tabhs_g_none_kernel(tc, tab, w4_words, w4_scales, w8, wgo, offs, o
 
         def up_pass(m, h):
             up = psum.tile([P, HALF], F32, name="up%d%d" % (m, h), tag="up%d%d" % (m, h))
-            nc.tensor.matmul_mx(
-                out=up[:],
-                lhsT=w8_codes[:, P * m : P * (m + 1)].bitcast(FP8X4),
-                lhsT_scale=w8_plane[:, P * m : P * (m + 1)],
-                rhs=got_words[h][:].bitcast(FP8X4),
-                rhs_scale=got_scales[h][:],
-                start=True,
-                stop=True,
-            )
+            for js in (slice(0, part), slice(part, HALF)):
+                nc.tensor.matmul_mx(
+                    out=up[:, js],
+                    lhsT=w8_codes[:, P * m : P * (m + 1)].bitcast(FP8X4),
+                    lhsT_scale=w8_plane[:, P * m : P * (m + 1)],
+                    rhs=got_words[h][:, js].bitcast(FP8X4),
+                    rhs_scale=got_scales[h][:, js],
+                    start=True,
+                    stop=True,
+                )
             weighted = keep.tile([P, HALF], F32, name="weighted%d%d" % (m, h))
             nc.vector.tensor_tensor(weighted[:], up[:], weights[:, h * HALF : (h + 1) * HALF], MULT)
             return weighted

@@ -1,7 +1,6 @@
 from contextlib import ExitStack
 
 import concourse.mybir as mybir
-from concourse.masks import make_identity
 
 K, M, T, S = 512, 256, 2048, 1024
 FLOPS = 2 * 2 * K * M * S
@@ -20,11 +19,9 @@ COPY = mybir.ActivationFunctionType.Copy
 
 P = 128
 PACK = 4
-HALF = 512
 STRIPE = 16
 GROUPS = 8
-HOLD = 8
-EARLY = 512
+SEG = 256
 
 
 def load_scale_rows(nc, plane, rows):
@@ -36,146 +33,162 @@ def tile_list_tabhs_g_none_kernel(tc, tab, w4_words, w4_scales, w8, wgo, offs, o
     nc = tc.nc
     with ExitStack() as ctx:
         keep = ctx.enter_context(tc.tile_pool(name="keep", bufs=1))
+        laid = ctx.enter_context(tc.tile_pool(name="laid", bufs=1))
         psum = ctx.enter_context(tc.psum_pool(name="psum", bufs=1))
+
+        words_at, plane_at, window_at = 0, 4 * T, 4 * T + M
+        raw_at = window_at + 4 * T
+        scales_at = raw_at + 2 * M + 4 * S
+        got_at = scales_at + T
+        late_at = got_at + 4 * S
 
         pick = keep.tile([P, S // STRIPE], U16, name="pick")
         nc.sync.dma_start(pick[:], offs)
-        tab_words = keep.tile([P, T], I32, name="tab_words", tag="shared", align_bytes=64)
-        words_hbm = tab[0, : K * T].bitcast(I32).rearrange("(p t) -> p t", p=P)
-        nc.sync.dma_start(out=tab_words[:, :EARLY], in_=words_hbm[:, :EARLY])
+        w8_raw = laid.tile([P, PACK, M], F32, name="w8_raw", offset=raw_at, align_bytes=64)
+        nc.sync.dma_start(out=w8_raw[:], in_=w8.rearrange("(p i) n -> p i n", i=PACK))
 
-        tab_scales = keep.tile([P, T // 4], I32, name="tab_scales", align_bytes=64)
+        tab_scales = laid.tile([P, T // 4], I32, name="tab_scales", offset=scales_at, align_bytes=64)
         nc.vector.memset(tab_scales[:], 0)
         load_scale_rows(nc, tab_scales, tab[0, K * T :].bitcast(I32).rearrange("(q t) -> q t", q=16))
 
-        w8_raw = keep.tile([P, PACK, M], F32, name="w8_raw")
-        nc.vector.memset(w8_raw[:, 0, :HOLD], 0.0)
-        nc.sync.dma_start(out=w8_raw[:], in_=w8.rearrange("(p i) n -> p i n", i=PACK))
-        nc.vector.memset(tab_words[:, EARLY : EARLY + HOLD], 0)
-        nc.sync.dma_start(out=tab_words[:, EARLY:], in_=words_hbm[:, EARLY:])
+        warm = keep.tile([P, 16], F32, name="warm")
+        nc.vector.memset(warm[:, :8], 0.0)
+        nc.scalar.activation(warm[:, 8:9], warm[:, 0:1], SILU)
 
-        w4 = keep.tile([P, M // 4 + M // 2], I32, name="w4", align_bytes=64)
-        w4_plane, w4_codes = w4[:, : M // 4], w4[:, M // 4 :]
-        nc.vector.memset(w4[:, : M // 4 + HOLD], 0)
-        nc.sync.dma_start(out=w4_codes, in_=w4_words[0].bitcast(I32))
+        w4_codes = keep.tile([P, M // 2], I32, name="w4_codes", align_bytes=64)
+        nc.sync.dma_start(out=w4_codes[:], in_=w4_words[0].bitcast(I32))
+        tab_words = laid.tile([P, T], I32, name="tab_words", offset=words_at, align_bytes=64)
+        nc.sync.dma_start(out=tab_words[:], in_=tab[0, : K * T].bitcast(I32).rearrange("(p t) -> p t", p=P))
+
+        w4_plane = laid.tile([P, M // 4], I32, name="w4_plane", offset=plane_at, align_bytes=64)
+        nc.vector.memset(w4_plane[:], 0)
         load_scale_rows(nc, w4_plane, w4_scales[0].bitcast(I32))
+        window0 = laid.tile([P, T], F32, name="window0", offset=window_at, align_bytes=64)
+        nc.vector.memset(window0[:].bitcast(I32), 0)
+        zeros = keep.tile([P, P], F32, name="zeros")
+        nc.vector.memset(zeros[:], 0.0)
+        ident = keep.tile([P, P], F32, name="ident")
+        nc.gpsimd.affine_select(
+            out=ident[:],
+            in_=zeros[:],
+            compare_op=mybir.AluOpType.not_equal,
+            fill=1.0,
+            base=0,
+            pattern=[[-1, P]],
+            channel_multiplier=1,
+        )
 
-        weights = keep.tile([P, S], F32, name="weights")
-        nc.vector.memset(weights[:, HALF - HOLD : HALF + HOLD], 0.0)
-        for h in range(2):
-            nc.sync.dma_start(out=weights[:, h * HALF : (h + 1) * HALF], in_=wgo[:, h * HALF : (h + 1) * HALF])
+        all_scales = keep.tile([P, S], U8, name="all_scales", align_bytes=64)
+        nc.vector.tensor_copy(all_scales[:], tab_scales[:].bitcast(U8).indirect(pick[:]))
+
+        w8_bf = laid.tile([P, M, PACK], BF16, name="w8_bf", offset=late_at - 4 * M, align_bytes=64)
+        nc.scalar.copy(w8_bf[:], w8_raw[:].rearrange("p i n -> p n i"))
+        w8_codes = laid.tile([P, M], U32, name="w8_codes", offset=scales_at, align_bytes=64)
+        w8_plane = laid.tile([P, M], U8, name="w8_plane", offset=scales_at + 4 * M, align_bytes=64)
+        nc.vector.quantize_mx(out=w8_codes[:].bitcast(FP8X4), scales=w8_plane[:], in_=w8_bf[:].rearrange("p n i -> p (n i)"))
+
+        weights = laid.tile([P, S], F32, name="weights", offset=raw_at, align_bytes=64)
+        for lo, hi in ((0, 2 * SEG), (2 * SEG, S)):
+            nc.sync.dma_start(out=weights[:, lo:hi], in_=wgo[:, lo:hi])
         place = keep.tile([P, S // STRIPE], U16, name="place")
         nc.sync.dma_start(place[:], offs2)
 
-        warm = keep.tile([P, 16], F32, name="warm")
-        nc.vector.memset(warm[:, :HOLD], 0.0)
-        nc.scalar.activation(warm[:, HOLD : HOLD + 1], warm[:, 0:1], SILU)
-        ident = keep.tile([P, P], F32, name="ident")
-        nc.vector.memset(ident[:, :HOLD], 0.0)
-        make_identity(nc, ident[:])
-
-        window0 = keep.tile([P, T], F32, name="window0")
-        nc.vector.memset(window0[:].bitcast(I32), 0)
-
-        cols = HALF // STRIPE
-        all_scales = keep.tile([P, S], U8, name="all_scales", align_bytes=64)
-        got_scales = [all_scales[:, h * HALF : (h + 1) * HALF] for h in range(2)]
-        got_words = [keep.tile([P, HALF], U32, name="got_words%d" % h, align_bytes=64) for h in range(2)]
-        nc.vector.tensor_copy(all_scales[:], tab_scales[:].bitcast(U8).indirect(pick[:]))
-
-        w8_bf = keep.tile([P, M, PACK], BF16, name="w8_bf", align_bytes=64)
-        nc.scalar.copy(w8_bf[:], w8_raw[:].rearrange("p i n -> p n i"))
-        w8_codes = keep.tile([P, M], U32, name="w8_codes", align_bytes=64)
-        w8_plane = keep.tile([P, M], U8, name="w8_plane", align_bytes=64)
-        nc.vector.quantize_mx(out=w8_codes[:].bitcast(FP8X4), scales=w8_plane[:], in_=w8_bf[:].rearrange("p n i -> p (n i)"))
-
-        part = HALF // 2
-        for lo, hi in ((0, part), (part, HALF), (HALF, S)):
+        got_words = laid.tile([P, S], U32, name="got_words", offset=got_at, align_bytes=64)
+        for lo, hi in ((0, SEG), (SEG, 2 * SEG), (2 * SEG, S)):
             nc.vector.tensor_copy(
-                got_words[lo // HALF][:, lo % HALF : lo % HALF + hi - lo],
-                tab_words[:].bitcast(U32).indirect(pick[:, lo // STRIPE : hi // STRIPE]),
+                got_words[:, lo:hi], tab_words[:].bitcast(U32).indirect(pick[:, lo // STRIPE : hi // STRIPE])
             )
 
-        window1 = keep.tile([P, T], F32, name="window1", tag="shared", align_bytes=64)
+        window1 = laid.tile([P, T], F32, name="window1", offset=late_at, align_bytes=64)
         nc.gpsimd.memset(window1[:], 0.0)
         windows = [window0, window1]
 
-        def gate_pass(m, h):
-            gate = psum.tile([P, HALF], F32, name="gate%d%d" % (m, h), tag="gate%d%d" % (m, h))
+        def project(dst, codes, plane, lo, hi):
             nc.tensor.matmul_mx(
-                out=gate[:],
-                lhsT=w4_codes.bitcast(U8)[:, 2 * P * m : 2 * P * (m + 1)].bitcast(FP4X4),
-                lhsT_scale=w4_plane.bitcast(U8)[:, P * m : P * (m + 1)],
-                rhs=got_words[h][:].bitcast(FP8X4),
-                rhs_scale=got_scales[h],
+                out=dst,
+                lhsT=codes,
+                lhsT_scale=plane,
+                rhs=got_words[:, lo:hi].bitcast(FP8X4),
+                rhs_scale=all_scales[:, lo:hi],
                 start=True,
                 stop=True,
             )
-            gated = keep.tile([P, HALF], F32, name="gated%d%d" % (m, h))
-            nc.scalar.activation(gated[:], gate[:], SILU)
-            return gated
 
-        def up_pass(m, h):
-            up = psum.tile([P, HALF], F32, name="up%d%d" % (m, h), tag="up%d%d" % (m, h))
-            for js in (slice(0, part), slice(part, HALF)):
-                nc.tensor.matmul_mx(
-                    out=up[:, js],
-                    lhsT=w8_codes[:, P * m : P * (m + 1)].bitcast(FP8X4),
-                    lhsT_scale=w8_plane[:, P * m : P * (m + 1)],
-                    rhs=got_words[h][:, js].bitcast(FP8X4),
-                    rhs_scale=got_scales[h][:, js],
-                    start=True,
-                    stop=True,
-                )
-            weighted = keep.tile([P, HALF], F32, name="weighted%d%d" % (m, h))
-            nc.vector.tensor_tensor(weighted[:], up[:], weights[:, h * HALF : (h + 1) * HALF], MULT)
-            return weighted
+        def gate_pass(dst, m, lo):
+            codes = w4_codes[:].bitcast(U8)[:, 2 * P * m : 2 * P * (m + 1)].bitcast(FP4X4)
+            project(dst, codes, w4_plane[:].bitcast(U8)[:, P * m : P * (m + 1)], lo, lo + SEG)
 
-        def scatter(m, h, gated, weighted):
+        gated = keep.tile([P, 2, S], F32, name="gated")
+        weighted = keep.tile([P, 2, S], F32, name="weighted")
+
+        def scatter(m, lo, hi):
             nc.vector.tensor_tensor(
-                windows[m][:].indirect(place[:, h * cols : (h + 1) * cols]), gated[:], weighted[:], MULT
+                windows[m][:].indirect(place[:, lo // STRIPE : hi // STRIPE]),
+                gated[:, m, lo:hi],
+                weighted[:, m, lo:hi],
+                MULT,
             )
 
-        first = [(up_pass(m, 0), gate_pass(m, 0)) for m in range(2)]
         for m in range(2):
-            scatter(m, 0, first[m][1], first[m][0])
+            gate = psum.tile([P, SEG], F32, name="gate%d" % m, tag="gate%d" % m)
+            gate_pass(gate[:], m, 0)
+            nc.scalar.activation(gated[:, m, :SEG], gate[:], SILU)
+            up = psum.tile([P, SEG], F32, name="up%d" % m, tag="up%d" % m)
+            project(up[:], w8_codes[:, P * m : P * (m + 1)].bitcast(FP8X4), w8_plane[:, P * m : P * (m + 1)], 0, SEG)
+            nc.vector.tensor_tensor(weighted[:, m, :SEG], up[:], weights[:, :SEG], MULT)
+            scatter(m, 0, SEG)
 
-        tiles = HALF // P
-        turned = psum.tile([P, tiles, P], F32, name="turned", tag="gate00")
-        for c in range(tiles):
-            nc.tensor.transpose(turned[:, c, :], weights[:, HALF + P * c : HALF + P * (c + 1)], ident[:])
-        token_weights = keep.tile([P, tiles, GROUPS], F32, name="token_weights")
-        nc.scalar.copy(token_weights[:], turned[:].rearrange("p c (g s) -> p c g s", s=STRIPE)[:, :, :, 0])
+        token_weights = keep.tile([P, S // P, GROUPS], F32, name="token_weights")
 
-        scaled = keep.tile([P, tiles, M], F32, name="scaled")
-        for pair in range(tiles // 2):
-            up_t = psum.tile([P, 2, M], F32, name="up_t%d" % pair, tag="gate%d0" % (1 - pair))
+        def turn_weights(first, last, tag):
+            turned = psum.tile([P, last - first, P], F32, name="turned%d" % first, tag=tag)
+            for c in range(first, last):
+                nc.tensor.transpose(turned[:, c - first, :], weights[:, P * c : P * (c + 1)], ident[:])
+            nc.scalar.copy(
+                token_weights[:, first:last, :], turned[:].rearrange("p c (g s) -> p c g s", s=STRIPE)[:, :, :, 0]
+            )
+
+        up_tags = ("gate1", "gate0", "gate1")
+        gate_tags = ("turn0", "turn1", "turn0")
+        back_tags = (("up0", "up1"), ("back0", "back1"), ("up0", "up1"))
+        turn_weights(2, 4, "turn0")
+        for seg in range(1, S // SEG):
+            lo, hi = seg * SEG, (seg + 1) * SEG
+            if seg == 2:
+                turn_weights(4, 8, "turn1")
+            up_t = psum.tile([P, 2, M], F32, name="up_t%d" % seg, tag=up_tags[seg - 1])
+            scaled = keep.tile([P, 2, 2, GROUPS, STRIPE], F32, name="scaled%d" % seg)
             for i in range(2):
-                c = 2 * pair + i
+                at = lo + P * i
                 nc.tensor.matmul_mx(
                     out=up_t[:, i, :],
-                    lhsT=got_words[1][:, P * c : P * (c + 1)].bitcast(FP8X4),
-                    lhsT_scale=got_scales[1][:, P * c : P * (c + 1)],
+                    lhsT=got_words[:, at : at + P].bitcast(FP8X4),
+                    lhsT_scale=all_scales[:, at : at + P],
                     rhs=w8_codes[:].bitcast(FP8X4),
                     rhs_scale=w8_plane[:],
                     start=True,
                     stop=True,
                 )
             for i in range(2):
-                c = 2 * pair + i
                 for g in range(GROUPS):
                     nc.scalar.activation(
-                        scaled[:, c, :].rearrange("p (m g s) -> p m g s", m=2, s=STRIPE)[:, :, g, :],
-                        up_t[:, i, :].rearrange("p (m g s) -> p m g s", m=2, s=STRIPE)[:, :, g, :],
+                        scaled[:, i, :, g, :],
+                        up_t[:, i, :].rearrange("p (m g s) -> p m g s", g=GROUPS, s=STRIPE)[:, :, g, :],
                         COPY,
-                        scale=token_weights[:, c, g : g + 1],
+                        scale=token_weights[:, 2 * seg + i, g : g + 1],
                     )
-        for m in range(2):
-            back = psum.tile([P, tiles, P], F32, name="back%d" % m, tag="up%d0" % m)
-            for c in range(tiles):
-                nc.tensor.transpose(back[:, c, :], scaled[:, c, P * m : P * (m + 1)], ident[:])
-            weighted = keep.tile([P, HALF], F32, name="weighted%d1" % m)
-            gated = gate_pass(m, 1)
-            nc.scalar.copy(weighted[:], back[:].rearrange("p c j -> p (c j)"))
-            scatter(m, 1, gated, weighted)
-            nc.sync.dma_start(out=out[P * m : P * (m + 1), :], in_=windows[m][:])
+            gates = psum.tile([P, 2, SEG], F32, name="gates%d" % seg, tag=gate_tags[seg - 1])
+            for m in range(2):
+                gate_pass(gates[:, m, :], m, lo)
+            nc.scalar.activation(gated[:, :, lo:hi], gates[:], SILU)
+            for m in range(2):
+                back = psum.tile([P, 2, P], F32, name="back%d_%d" % (seg, m), tag=back_tags[seg - 1][m])
+                for i in range(2):
+                    nc.tensor.transpose(back[:, i, :], scaled[:, i, m].rearrange("p g s -> p (g s)"), ident[:])
+                nc.scalar.copy(weighted[:, m, lo:hi], back[:].rearrange("p i j -> p (i j)"))
+            scatter(0, lo, hi)
+            if seg == 1:
+                scatter(1, lo, hi)
+        nc.sync.dma_start(out=out[:P, :], in_=window0[:])
+        scatter(1, 2 * SEG, S)
+        nc.sync.dma_start(out=out[P:, :], in_=window1[:])

@@ -22,11 +22,12 @@ PACK = 4
 STRIPE = 16
 GROUPS = 8
 SEG = 256
+EARLY = 512
 
 
 def load_scale_rows(nc, plane, rows):
-    for q in range(4):
-        nc.sync.dma_start(out=plane[32 * q : 32 * q + 4, :], in_=rows[4 * q : 4 * q + 4, :])
+    for r in range(4):
+        nc.sync.dma_start(out=plane[r:P:32, :], in_=rows[r:16:4, :])
 
 
 def tile_list_tabhs_g_none_kernel(tc, tab, w4_words, w4_scales, w8, wgo, offs, offs2, out):
@@ -44,8 +45,9 @@ def tile_list_tabhs_g_none_kernel(tc, tab, w4_words, w4_scales, w8, wgo, offs, o
 
         pick = keep.tile([P, S // STRIPE], U16, name="pick")
         nc.sync.dma_start(pick[:], offs)
-        w8_raw = laid.tile([P, PACK, M], F32, name="w8_raw", offset=raw_at, align_bytes=64)
-        nc.sync.dma_start(out=w8_raw[:], in_=w8.rearrange("(p i) n -> p i n", i=PACK))
+        tab_words = laid.tile([P, T], I32, name="tab_words", offset=words_at, align_bytes=64)
+        words_hbm = tab[0, : K * T].bitcast(I32).rearrange("(p t) -> p t", p=P)
+        nc.sync.dma_start(out=tab_words[:, :EARLY], in_=words_hbm[:, :EARLY])
 
         tab_scales = laid.tile([P, T // 4], I32, name="tab_scales", offset=scales_at, align_bytes=64)
         nc.vector.memset(tab_scales[:], 0)
@@ -55,10 +57,11 @@ def tile_list_tabhs_g_none_kernel(tc, tab, w4_words, w4_scales, w8, wgo, offs, o
         nc.vector.memset(warm[:, :8], 0.0)
         nc.scalar.activation(warm[:, 8:9], warm[:, 0:1], SILU)
 
+        w8_raw = laid.tile([P, PACK, M], F32, name="w8_raw", offset=raw_at, align_bytes=64)
+        nc.sync.dma_start(out=w8_raw[:], in_=w8.rearrange("(p i) n -> p i n", i=PACK))
+        nc.sync.dma_start(out=tab_words[:, EARLY:], in_=words_hbm[:, EARLY:])
         w4_codes = keep.tile([P, M // 2], I32, name="w4_codes", align_bytes=64)
         nc.sync.dma_start(out=w4_codes[:], in_=w4_words[0].bitcast(I32))
-        tab_words = laid.tile([P, T], I32, name="tab_words", offset=words_at, align_bytes=64)
-        nc.sync.dma_start(out=tab_words[:], in_=tab[0, : K * T].bitcast(I32).rearrange("(p t) -> p t", p=P))
 
         w4_plane = laid.tile([P, M // 4], I32, name="w4_plane", offset=plane_at, align_bytes=64)
         nc.vector.memset(w4_plane[:], 0)

@@ -23,6 +23,7 @@ STRIPE = 16
 GROUPS = 8
 SEG = 256
 EARLY = 512
+LAST = 384
 
 
 def load_scale_rows(nc, plane, rows):
@@ -85,7 +86,9 @@ def tile_list_tabhs_g_none_kernel(tc, tab, w4_words, w4_scales, w8, wgo, offs, o
         nc.vector.tensor_copy(all_scales[:], tab_scales[:].bitcast(U8).indirect(pick[:]))
 
         w8_bf = laid.tile([P, M, PACK], BF16, name="w8_bf", offset=late_at - 4 * M, align_bytes=64)
-        nc.scalar.copy(w8_bf[:], w8_raw[:].rearrange("p i n -> p n i"))
+        nc.scalar.copy(
+            w8_bf[:].rearrange("p (c j) i -> p c i j", j=PACK), w8_raw[:].rearrange("p i (c j) -> p c i j", j=PACK)
+        )
         w8_codes = laid.tile([P, M], U32, name="w8_codes", offset=scales_at, align_bytes=64)
         w8_plane = laid.tile([P, M], U8, name="w8_plane", offset=scales_at + 4 * M, align_bytes=64)
         nc.vector.quantize_mx(out=w8_codes[:].bitcast(FP8X4), scales=w8_plane[:], in_=w8_bf[:].rearrange("p n i -> p (n i)"))
@@ -190,8 +193,8 @@ def tile_list_tabhs_g_none_kernel(tc, tab, w4_words, w4_scales, w8, wgo, offs, o
                     nc.tensor.transpose(back[:, i, :], scaled[:, i, m].rearrange("p g s -> p (g s)"), ident[:])
                 nc.scalar.copy(weighted[:, m, lo:hi], back[:].rearrange("p i j -> p (i j)"))
             scatter(0, lo, hi)
-            if seg == 1:
-                scatter(1, lo, hi)
+            if seg < 3:
+                scatter(1, lo, min(hi, S - LAST))
         nc.sync.dma_start(out=out[:P, :], in_=window0[:])
-        scatter(1, 2 * SEG, S)
+        scatter(1, S - LAST, S)
         nc.sync.dma_start(out=out[P:, :], in_=window1[:])

@@ -22,7 +22,6 @@ PACK = 4
 STRIPE = 16
 GROUPS = 8
 SEG = 256
-EARLY = 512
 LAST = 384
 
 
@@ -35,22 +34,15 @@ def tile_list_tabhs_g_none_kernel(tc, tab, w4_words, w4_scales, w8, wgo, offs, o
     nc = tc.nc
     with ExitStack() as ctx:
         keep = ctx.enter_context(tc.tile_pool(name="keep", bufs=1))
-        laid = ctx.enter_context(tc.tile_pool(name="laid", bufs=1))
         psum = ctx.enter_context(tc.psum_pool(name="psum", bufs=1))
-
-        words_at, plane_at, window_at = 0, 4 * T, 4 * T + M
-        raw_at = window_at + 4 * T
-        scales_at = raw_at + 2 * M + 4 * S
-        got_at = scales_at + T
-        late_at = got_at + 4 * S
 
         pick = keep.tile([P, S // STRIPE], U16, name="pick")
         nc.sync.dma_start(pick[:], offs)
-        tab_words = laid.tile([P, T], I32, name="tab_words", offset=words_at, align_bytes=64)
-        words_hbm = tab[0, : K * T].bitcast(I32).rearrange("(p t) -> p t", p=P)
-        nc.sync.dma_start(out=tab_words[:, :EARLY], in_=words_hbm[:, :EARLY])
+        w8_raw = keep.tile([P, PACK, M], F32, name="w8_raw")
+        w8_rows = w8.rearrange("(p i) n -> p i n", i=PACK)
+        nc.sync.dma_start(out=w8_raw[:, :2, :], in_=w8_rows[:, :2, :])
 
-        tab_scales = laid.tile([P, T // 4], I32, name="tab_scales", offset=scales_at, align_bytes=64)
+        tab_scales = keep.tile([P, T // 4], I32, name="tab_scales", align_bytes=64)
         nc.vector.memset(tab_scales[:], 0)
         load_scale_rows(nc, tab_scales, tab[0, K * T :].bitcast(I32).rearrange("(q t) -> q t", q=16))
 
@@ -58,16 +50,16 @@ def tile_list_tabhs_g_none_kernel(tc, tab, w4_words, w4_scales, w8, wgo, offs, o
         nc.vector.memset(warm[:, :8], 0.0)
         nc.scalar.activation(warm[:, 8:9], warm[:, 0:1], SILU)
 
-        w8_raw = laid.tile([P, PACK, M], F32, name="w8_raw", offset=raw_at, align_bytes=64)
-        nc.sync.dma_start(out=w8_raw[:], in_=w8.rearrange("(p i) n -> p i n", i=PACK))
-        nc.sync.dma_start(out=tab_words[:, EARLY:], in_=words_hbm[:, EARLY:])
+        nc.sync.dma_start(out=w8_raw[:, 2:, :], in_=w8_rows[:, 2:, :])
+        tab_words = keep.tile([P, T], I32, name="tab_words", align_bytes=64)
+        nc.sync.dma_start(out=tab_words[:], in_=tab[0, : K * T].bitcast(I32).rearrange("(p t) -> p t", p=P))
         w4_codes = keep.tile([P, M // 2], I32, name="w4_codes", align_bytes=64)
         nc.sync.dma_start(out=w4_codes[:], in_=w4_words[0].bitcast(I32))
 
-        w4_plane = laid.tile([P, M // 4], I32, name="w4_plane", offset=plane_at, align_bytes=64)
+        w4_plane = keep.tile([P, M // 4], I32, name="w4_plane", align_bytes=64)
         nc.vector.memset(w4_plane[:], 0)
         load_scale_rows(nc, w4_plane, w4_scales[0].bitcast(I32))
-        window0 = laid.tile([P, T], F32, name="window0", offset=window_at, align_bytes=64)
+        window0 = keep.tile([P, T], F32, name="window0", align_bytes=64)
         nc.vector.memset(window0[:].bitcast(I32), 0)
         zeros = keep.tile([P, P], F32, name="zeros")
         nc.vector.memset(zeros[:], 0.0)
@@ -85,27 +77,27 @@ def tile_list_tabhs_g_none_kernel(tc, tab, w4_words, w4_scales, w8, wgo, offs, o
         all_scales = keep.tile([P, S], U8, name="all_scales", align_bytes=64)
         nc.vector.tensor_copy(all_scales[:], tab_scales[:].bitcast(U8).indirect(pick[:]))
 
-        w8_bf = laid.tile([P, M, PACK], BF16, name="w8_bf", offset=late_at - 4 * M, align_bytes=64)
+        w8_bf = keep.tile([P, M, PACK], BF16, name="w8_bf", tag="late", align_bytes=64)
         nc.scalar.copy(
             w8_bf[:].rearrange("p (c j) i -> p c i j", j=PACK), w8_raw[:].rearrange("p i (c j) -> p c i j", j=PACK)
         )
-        w8_codes = laid.tile([P, M], U32, name="w8_codes", offset=scales_at, align_bytes=64)
-        w8_plane = laid.tile([P, M], U8, name="w8_plane", offset=scales_at + 4 * M, align_bytes=64)
+        w8_codes = keep.tile([P, M], U32, name="w8_codes", align_bytes=64)
+        w8_plane = keep.tile([P, M], U8, name="w8_plane", align_bytes=64)
         nc.vector.quantize_mx(out=w8_codes[:].bitcast(FP8X4), scales=w8_plane[:], in_=w8_bf[:].rearrange("p n i -> p (n i)"))
 
-        weights = laid.tile([P, S], F32, name="weights", offset=raw_at, align_bytes=64)
+        weights = keep.tile([P, S], F32, name="weights", align_bytes=64)
         for lo, hi in ((0, 2 * SEG), (2 * SEG, S)):
             nc.sync.dma_start(out=weights[:, lo:hi], in_=wgo[:, lo:hi])
         place = keep.tile([P, S // STRIPE], U16, name="place")
         nc.sync.dma_start(place[:], offs2)
 
-        got_words = laid.tile([P, S], U32, name="got_words", offset=got_at, align_bytes=64)
+        got_words = keep.tile([P, S], U32, name="got_words", align_bytes=64)
         for lo, hi in ((0, SEG), (SEG, 2 * SEG), (2 * SEG, S)):
             nc.vector.tensor_copy(
                 got_words[:, lo:hi], tab_words[:].bitcast(U32).indirect(pick[:, lo // STRIPE : hi // STRIPE])
             )
 
-        window1 = laid.tile([P, T], F32, name="window1", offset=late_at, align_bytes=64)
+        window1 = keep.tile([P, T], F32, name="window1", tag="late", align_bytes=64)
         nc.gpsimd.memset(window1[:], 0.0)
         windows = [window0, window1]
 

@@ -146,7 +146,7 @@ def tile_list_tabhs_g_none_kernel(tc, tab, w4_words, w4_scales, w8, wgo, offs, o
                 token_weights[:, first:last, :], turned[:].rearrange("p c (g s) -> p c g s", s=STRIPE)[:, :, :, 0]
             )
 
-        up_tags = ("gate1", "gate0", "gate1")
+        up_tags = ("gate0", "gate1", "gate0")
         gate_tags = ("turn0", "turn1", "turn0")
         back_tags = (("up0", "up1"), ("back0", "back1"), ("up0", "up1"))
         turn_weights(2, 4, "turn0")

@@ -23,11 +23,12 @@ STRIPE = 16
 GROUPS = 8
 SEG = 256
 LAST = 384
+HALF = S // 2
 
 
-def load_scale_rows(nc, plane, rows):
-    for r in range(4):
-        nc.sync.dma_start(out=plane[r:P:32, :], in_=rows[r:16:4, :])
+def load_scale_rows(queue, plane, rows, which=range(4)):
+    for r in which:
+        queue.dma_start(out=plane[r:P:32, :], in_=rows[r])
 
 
 def tile_list_tabhs_g_none_kernel(tc, tab, w4_words, w4_scales, w8, wgo, offs, offs2, out):
@@ -38,27 +39,37 @@ def tile_list_tabhs_g_none_kernel(tc, tab, w4_words, w4_scales, w8, wgo, offs, o
 
         pick = keep.tile([P, S // STRIPE], U16, name="pick")
         nc.sync.dma_start(pick[:], offs)
-        w8_raw = keep.tile([P, PACK, M], F32, name="w8_raw")
+        w8_raw = keep.tile([P, PACK, M], F32, name="w8_raw", tag="raw", align_bytes=64)
         w8_rows = w8.rearrange("(p i) n -> p i n", i=PACK)
         nc.sync.dma_start(out=w8_raw[:, :2, :], in_=w8_rows[:, :2, :])
 
         tab_scales = keep.tile([P, T // 4], I32, name="tab_scales", align_bytes=64)
         nc.vector.memset(tab_scales[:], 0)
-        load_scale_rows(nc, tab_scales, tab[0, K * T :].bitcast(I32).rearrange("(q t) -> q t", q=16))
+        nc.sync.dma_start(out=tab_scales[0:P:8, :], in_=tab[0, K * T :].bitcast(I32).rearrange("(q t) -> q t", q=16))
+
+        w4_plane = keep.tile([P, M // 4], I32, name="w4_plane", align_bytes=64)
+        nc.vector.memset(w4_plane[:], 0)
 
         warm = keep.tile([P, 16], F32, name="warm")
         nc.vector.memset(warm[:, :8], 0.0)
         nc.scalar.activation(warm[:, 8:9], warm[:, 0:1], SILU)
 
         nc.sync.dma_start(out=w8_raw[:, 2:, :], in_=w8_rows[:, 2:, :])
-        tab_words = keep.tile([P, T], I32, name="tab_words", align_bytes=64)
-        nc.sync.dma_start(out=tab_words[:], in_=tab[0, : K * T].bitcast(I32).rearrange("(p t) -> p t", p=P))
         w4_codes = keep.tile([P, M // 2], I32, name="w4_codes", align_bytes=64)
         nc.sync.dma_start(out=w4_codes[:], in_=w4_words[0].bitcast(I32))
+        w4_rows = [w4_scales[0].bitcast(I32)[r:16:4, :] for r in range(4)]
+        load_scale_rows(nc.sync, w4_plane, w4_rows, (0, 1))
+        tab_words = keep.tile([P, T], I32, name="tab_words", align_bytes=64)
+        nc.sync.dma_start(out=tab_words[:], in_=tab[0, : K * T].bitcast(I32).rearrange("(p t) -> p t", p=P))
+        load_scale_rows(nc.sync, w4_plane, w4_rows, (2, 3))
 
-        w4_plane = keep.tile([P, M // 4], I32, name="w4_plane", align_bytes=64)
-        nc.vector.memset(w4_plane[:], 0)
-        load_scale_rows(nc, w4_plane, w4_scales[0].bitcast(I32))
+        got_planes = [keep.tile([P, HALF // 4], I32, name="got_plane%d" % h, align_bytes=64) for h in range(2)]
+        for plane in got_planes:
+            nc.vector.memset(plane[:], 0)
+
+        def scales_of(lo, hi):
+            return got_planes[lo // HALF][:].bitcast(U8)[:, lo % HALF : lo % HALF + hi - lo]
+
         window0 = keep.tile([P, T], F32, name="window0", align_bytes=64)
         nc.vector.memset(window0[:].bitcast(I32), 0)
         zeros = keep.tile([P, P], F32, name="zeros")
@@ -74,8 +85,23 @@ def tile_list_tabhs_g_none_kernel(tc, tab, w4_words, w4_scales, w8, wgo, offs, o
             channel_multiplier=1,
         )
 
-        all_scales = keep.tile([P, S], U8, name="all_scales", align_bytes=64)
-        nc.vector.tensor_copy(all_scales[:], tab_scales[:].bitcast(U8).indirect(pick[:]))
+
+        weights = keep.tile([P, S], F32, name="weights", align_bytes=64)
+        place = keep.tile([P, S // STRIPE], U16, name="place")
+
+        for lo, hi in ((0, S // 2), (S // 2, S)):
+            nc.sync.dma_start(out=weights[:, lo:hi], in_=wgo[:, lo:hi])
+            got_scales = keep.tile([P, HALF], U8, name="got_scales%d" % lo, align_bytes=64)
+            nc.vector.tensor_copy(
+                got_scales[:], tab_scales[:].bitcast(U8).indirect(pick[:, lo // STRIPE : hi // STRIPE])
+            )
+            load_scale_rows(
+                nc.sync,
+                got_planes[lo // HALF],
+                [got_scales[8 * r : P : 32, :].bitcast(I32) for r in range(4)],
+            )
+            if lo == 0:
+                nc.sync.dma_start(place[:], offs2)
 
         w8_bf = keep.tile([P, M, PACK], BF16, name="w8_bf", tag="late", align_bytes=64)
         nc.scalar.copy(
@@ -85,13 +111,7 @@ def tile_list_tabhs_g_none_kernel(tc, tab, w4_words, w4_scales, w8, wgo, offs, o
         w8_plane = keep.tile([P, M], U8, name="w8_plane", align_bytes=64)
         nc.vector.quantize_mx(out=w8_codes[:].bitcast(FP8X4), scales=w8_plane[:], in_=w8_bf[:].rearrange("p n i -> p (n i)"))
 
-        weights = keep.tile([P, S], F32, name="weights", align_bytes=64)
-        for lo, hi in ((0, 2 * SEG), (2 * SEG, S)):
-            nc.sync.dma_start(out=weights[:, lo:hi], in_=wgo[:, lo:hi])
-        place = keep.tile([P, S // STRIPE], U16, name="place")
-        nc.sync.dma_start(place[:], offs2)
-
-        got_words = keep.tile([P, S], U32, name="got_words", align_bytes=64)
+        got_words = keep.tile([P, S], U32, name="got_words", tag="raw", align_bytes=64)
         for lo, hi in ((0, SEG), (SEG, 2 * SEG), (2 * SEG, S)):
             nc.vector.tensor_copy(
                 got_words[:, lo:hi], tab_words[:].bitcast(U32).indirect(pick[:, lo // STRIPE : hi // STRIPE])
@@ -107,7 +127,7 @@ def tile_list_tabhs_g_none_kernel(tc, tab, w4_words, w4_scales, w8, wgo, offs, o
                 lhsT=codes,
                 lhsT_scale=plane,
                 rhs=got_words[:, lo:hi].bitcast(FP8X4),
-                rhs_scale=all_scales[:, lo:hi],
+                rhs_scale=scales_of(lo, hi),
                 start=True,
                 stop=True,
             )
@@ -161,7 +181,7 @@ def tile_list_tabhs_g_none_kernel(tc, tab, w4_words, w4_scales, w8, wgo, offs, o
                 nc.tensor.matmul_mx(
                     out=up_t[:, i, :],
                     lhsT=got_words[:, at : at + P].bitcast(FP8X4),
-                    lhsT_scale=all_scales[:, at : at + P],
+                    lhsT_scale=scales_of(at, at + P),
                     rhs=w8_codes[:].bitcast(FP8X4),
                     rhs_scale=w8_plane[:],
                     start=True,

@@ -41,7 +41,7 @@ def tile_list_tabhs_g_none_kernel(tc, tab, w4_words, w4_scales, w8, wgo, offs, o
         nc.sync.dma_start(pick[:], offs)
         w8_raw = keep.tile([P, PACK, M], F32, name="w8_raw", tag="raw", align_bytes=64)
         w8_rows = w8.rearrange("(p i) n -> p i n", i=PACK)
-        nc.sync.dma_start(out=w8_raw[:, :2, :], in_=w8_rows[:, :2, :])
+        nc.sync.dma_start(out=w8_raw[:, :1, :], in_=w8_rows[:, :1, :])
 
         tab_scales = keep.tile([P, T // 4], I32, name="tab_scales", align_bytes=64)
         nc.vector.memset(tab_scales[:], 0)
@@ -54,14 +54,14 @@ def tile_list_tabhs_g_none_kernel(tc, tab, w4_words, w4_scales, w8, wgo, offs, o
         nc.vector.memset(warm[:, :8], 0.0)
         nc.scalar.activation(warm[:, 8:9], warm[:, 0:1], SILU)
 
-        nc.sync.dma_start(out=w8_raw[:, 2:, :], in_=w8_rows[:, 2:, :])
-        w4_codes = keep.tile([P, M // 2], I32, name="w4_codes", align_bytes=64)
-        nc.sync.dma_start(out=w4_codes[:], in_=w4_words[0].bitcast(I32))
+        nc.sync.dma_start(out=w8_raw[:, 1:, :], in_=w8_rows[:, 1:, :])
         w4_rows = [w4_scales[0].bitcast(I32)[r:16:4, :] for r in range(4)]
-        load_scale_rows(nc.sync, w4_plane, w4_rows, (0, 1))
+        load_scale_rows(nc.sync, w4_plane, w4_rows, (0, 1, 2))
         tab_words = keep.tile([P, T], I32, name="tab_words", align_bytes=64)
         nc.sync.dma_start(out=tab_words[:], in_=tab[0, : K * T].bitcast(I32).rearrange("(p t) -> p t", p=P))
-        load_scale_rows(nc.sync, w4_plane, w4_rows, (2, 3))
+        w4_codes = keep.tile([P, M // 2], I32, name="w4_codes", align_bytes=64)
+        nc.sync.dma_start(out=w4_codes[:], in_=w4_words[0].bitcast(I32))
+        load_scale_rows(nc.sync, w4_plane, w4_rows, (3,))
 
         got_planes = [keep.tile([P, HALF // 4], I32, name="got_plane%d" % h, align_bytes=64) for h in range(2)]
         for plane in got_planes:
@@ -154,6 +154,7 @@ def tile_list_tabhs_g_none_kernel(tc, tab, w4_words, w4_scales, w8, wgo, offs, o
             up = psum.tile([P, SEG], F32, name="up%d" % m, tag="up%d" % m)
             project(up[:], w8_codes[:, P * m : P * (m + 1)].bitcast(FP8X4), w8_plane[:, P * m : P * (m + 1)], 0, SEG)
             nc.vector.tensor_tensor(weighted[:, m, :SEG], up[:], weights[:, :SEG], MULT)
+        for m in range(2):
             scatter(m, 0, SEG)
 
         token_weights = keep.tile([P, S // P, GROUPS], F32, name="token_weights")

@@ -37,15 +37,15 @@ def tile_list_tabhs_g_none_kernel(tc, tab, w4_words, w4_scales, w8, wgo, offs, o
         keep = ctx.enter_context(tc.tile_pool(name="keep", bufs=1))
         psum = ctx.enter_context(tc.psum_pool(name="psum", bufs=1))
 
-        pick = keep.tile([P, S // STRIPE], U16, name="pick")
-        nc.sync.dma_start(pick[:], offs)
         w8_raw = keep.tile([P, PACK, M], F32, name="w8_raw", tag="raw", align_bytes=64)
         w8_rows = w8.rearrange("(p i) n -> p i n", i=PACK)
-        nc.sync.dma_start(out=w8_raw[:, :1, :], in_=w8_rows[:, :1, :])
 
         tab_scales = keep.tile([P, T // 4], I32, name="tab_scales", align_bytes=64)
-        nc.vector.memset(tab_scales[:], 0)
-        nc.sync.dma_start(out=tab_scales[0:P:8, :], in_=tab[0, K * T :].bitcast(I32).rearrange("(q t) -> q t", q=16))
+        nc.vector.memset(tab_scales[: P - 16, :], 0)
+        nc.sync.dma_start(out=tab_scales[P - 16 :, :], in_=tab[0, K * T :].bitcast(I32).rearrange("(q t) -> q t", q=16))
+
+        pick = keep.tile([P, S // STRIPE], U16, name="pick")
+        nc.sync.dma_start(pick[:], offs)
 
         w4_plane = keep.tile([P, M // 4], I32, name="w4_plane", align_bytes=64)
         nc.vector.memset(w4_plane[:], 0)
@@ -54,14 +54,13 @@ def tile_list_tabhs_g_none_kernel(tc, tab, w4_words, w4_scales, w8, wgo, offs, o
         nc.vector.memset(warm[:, :8], 0.0)
         nc.scalar.activation(warm[:, 8:9], warm[:, 0:1], SILU)
 
-        nc.sync.dma_start(out=w8_raw[:, 1:, :], in_=w8_rows[:, 1:, :])
+        nc.sync.dma_start(out=w8_raw[:], in_=w8_rows)
         w4_rows = [w4_scales[0].bitcast(I32)[r:16:4, :] for r in range(4)]
-        load_scale_rows(nc.sync, w4_plane, w4_rows, (0, 1, 2))
+        load_scale_rows(nc.sync, w4_plane, w4_rows)
         tab_words = keep.tile([P, T], I32, name="tab_words", align_bytes=64)
         nc.sync.dma_start(out=tab_words[:], in_=tab[0, : K * T].bitcast(I32).rearrange("(p t) -> p t", p=P))
         w4_codes = keep.tile([P, M // 2], I32, name="w4_codes", align_bytes=64)
         nc.sync.dma_start(out=w4_codes[:], in_=w4_words[0].bitcast(I32))
-        load_scale_rows(nc.sync, w4_plane, w4_rows, (3,))
 
         got_planes = [keep.tile([P, HALF // 4], I32, name="got_plane%d" % h, align_bytes=64) for h in range(2)]
         for plane in got_planes:
@@ -70,9 +69,7 @@ def tile_list_tabhs_g_none_kernel(tc, tab, w4_words, w4_scales, w8, wgo, offs, o
         def scales_of(lo, hi):
             return got_planes[lo // HALF][:].bitcast(U8)[:, lo % HALF : lo % HALF + hi - lo]
 
-        window0 = keep.tile([P, T], F32, name="window0", align_bytes=64)
-        nc.vector.memset(window0[:].bitcast(I32), 0)
-        zeros = keep.tile([P, P], F32, name="zeros")
+        zeros = keep.tile([P, P], F32, name="zeros", tag="early", align_bytes=64)
         nc.vector.memset(zeros[:], 0.0)
         ident = keep.tile([P, P], F32, name="ident")
         nc.gpsimd.affine_select(
@@ -90,7 +87,6 @@ def tile_list_tabhs_g_none_kernel(tc, tab, w4_words, w4_scales, w8, wgo, offs, o
         place = keep.tile([P, S // STRIPE], U16, name="place")
 
         for lo, hi in ((0, S // 2), (S // 2, S)):
-            nc.sync.dma_start(out=weights[:, lo:hi], in_=wgo[:, lo:hi])
             got_scales = keep.tile([P, HALF], U8, name="got_scales%d" % lo, align_bytes=64)
             nc.vector.tensor_copy(
                 got_scales[:], tab_scales[:].bitcast(U8).indirect(pick[:, lo // STRIPE : hi // STRIPE])
@@ -98,10 +94,12 @@ def tile_list_tabhs_g_none_kernel(tc, tab, w4_words, w4_scales, w8, wgo, offs, o
             load_scale_rows(
                 nc.sync,
                 got_planes[lo // HALF],
-                [got_scales[8 * r : P : 32, :].bitcast(I32) for r in range(4)],
+                [got_scales[P - 16 + r : P : 4, :].bitcast(I32) for r in range(4)],
             )
             if lo == 0:
+                nc.sync.dma_start(out=weights[:, :HALF], in_=wgo[:, :HALF])
                 nc.sync.dma_start(place[:], offs2)
+                nc.sync.dma_start(out=weights[:, HALF:], in_=wgo[:, HALF:])
 
         w8_bf = keep.tile([P, M, PACK], BF16, name="w8_bf", tag="late", align_bytes=64)
         nc.scalar.copy(
@@ -117,7 +115,9 @@ def tile_list_tabhs_g_none_kernel(tc, tab, w4_words, w4_scales, w8, wgo, offs, o
                 got_words[:, lo:hi], tab_words[:].bitcast(U32).indirect(pick[:, lo // STRIPE : hi // STRIPE])
             )
 
-        window1 = keep.tile([P, T], F32, name="window1", tag="late", align_bytes=64)
+        window0 = keep.tile([P, T], F32, name="window0", tag="late", align_bytes=64)
+        nc.gpsimd.memset(window0[:], 0.0)
+        window1 = keep.tile([P, T], F32, name="window1", tag="early", align_bytes=64)
         nc.gpsimd.memset(window1[:], 0.0)
         windows = [window0, window1]
 

@@ -40,6 +40,7 @@ def tile_list_tabhs_g_none_kernel(tc, tab, w4_words, w4_scales, w8, wgo, offs, o
         w8_raw = keep.tile([P, PACK, M], F32, name="w8_raw", tag="raw", align_bytes=64)
         w8_rows = w8.rearrange("(p i) n -> p i n", i=PACK)
 
+        nc.sync.dma_start(out=w8_raw[:, :1, :], in_=w8_rows[:, :1, :])
         tab_scales = keep.tile([P, T // 4], I32, name="tab_scales", align_bytes=64)
         nc.vector.memset(tab_scales[: P - 16, :], 0)
         nc.sync.dma_start(out=tab_scales[P - 16 :, :], in_=tab[0, K * T :].bitcast(I32).rearrange("(q t) -> q t", q=16))
@@ -54,13 +55,14 @@ def tile_list_tabhs_g_none_kernel(tc, tab, w4_words, w4_scales, w8, wgo, offs, o
         nc.vector.memset(warm[:, :8], 0.0)
         nc.scalar.activation(warm[:, 8:9], warm[:, 0:1], SILU)
 
-        nc.sync.dma_start(out=w8_raw[:], in_=w8_rows)
+        nc.sync.dma_start(out=w8_raw[:, 1:, :], in_=w8_rows[:, 1:, :])
         w4_rows = [w4_scales[0].bitcast(I32)[r:16:4, :] for r in range(4)]
-        load_scale_rows(nc.sync, w4_plane, w4_rows)
+        load_scale_rows(nc.sync, w4_plane, w4_rows, (0, 1, 2))
         tab_words = keep.tile([P, T], I32, name="tab_words", align_bytes=64)
         nc.sync.dma_start(out=tab_words[:], in_=tab[0, : K * T].bitcast(I32).rearrange("(p t) -> p t", p=P))
         w4_codes = keep.tile([P, M // 2], I32, name="w4_codes", align_bytes=64)
         nc.sync.dma_start(out=w4_codes[:], in_=w4_words[0].bitcast(I32))
+        load_scale_rows(nc.sync, w4_plane, w4_rows, (3,))
 
         got_planes = [keep.tile([P, HALF // 4], I32, name="got_plane%d" % h, align_bytes=64) for h in range(2)]
         for plane in got_planes:
@@ -87,6 +89,7 @@ def tile_list_tabhs_g_none_kernel(tc, tab, w4_words, w4_scales, w8, wgo, offs, o
         place = keep.tile([P, S // STRIPE], U16, name="place")
 
         for lo, hi in ((0, S // 2), (S // 2, S)):
+            nc.sync.dma_start(out=weights[:, lo:hi], in_=wgo[:, lo:hi])
             got_scales = keep.tile([P, HALF], U8, name="got_scales%d" % lo, align_bytes=64)
             nc.vector.tensor_copy(
                 got_scales[:], tab_scales[:].bitcast(U8).indirect(pick[:, lo // STRIPE : hi // STRIPE])
@@ -97,9 +100,7 @@ def tile_list_tabhs_g_none_kernel(tc, tab, w4_words, w4_scales, w8, wgo, offs, o
                 [got_scales[P - 16 + r : P : 4, :].bitcast(I32) for r in range(4)],
             )
             if lo == 0:
-                nc.sync.dma_start(out=weights[:, :HALF], in_=wgo[:, :HALF])
                 nc.sync.dma_start(place[:], offs2)
-                nc.sync.dma_start(out=weights[:, HALF:], in_=wgo[:, HALF:])
 
         w8_bf = keep.tile([P, M, PACK], BF16, name="w8_bf", tag="late", align_bytes=64)
         nc.scalar.copy(

@@ -149,12 +149,12 @@ def tile_list_tabhs_g_none_kernel(tc, tab, w4_words, w4_scales, w8, wgo, offs, o
             )
 
         for m in range(2):
-            gate = psum.tile([P, SEG], F32, name="gate%d" % m, tag="gate%d" % m)
-            gate_pass(gate[:], m, 0)
-            nc.scalar.activation(gated[:, m, :SEG], gate[:], SILU)
             up = psum.tile([P, SEG], F32, name="up%d" % m, tag="up%d" % m)
             project(up[:], w8_codes[:, P * m : P * (m + 1)].bitcast(FP8X4), w8_plane[:, P * m : P * (m + 1)], 0, SEG)
             nc.vector.tensor_tensor(weighted[:, m, :SEG], up[:], weights[:, :SEG], MULT)
+            gate = psum.tile([P, SEG], F32, name="gate%d" % m, tag="gate%d" % m)
+            gate_pass(gate[:], m, 0)
+            nc.scalar.activation(gated[:, m, :SEG], gate[:], SILU)
         for m in range(2):
             scatter(m, 0, SEG)
 
@@ -168,10 +168,10 @@ def tile_list_tabhs_g_none_kernel(tc, tab, w4_words, w4_scales, w8, wgo, offs, o
                 token_weights[:, first:last, :], turned[:].rearrange("p c (g s) -> p c g s", s=STRIPE)[:, :, :, 0]
             )
 
-        up_tags = ("gate0", "gate1", "gate0")
-        gate_tags = ("turn0", "turn1", "turn0")
+        up_tags = ("turn0", "gate1", "turn0")
+        gate_tags = ("gate0", "turn1", "gate0")
         back_tags = (("up0", "up1"), ("back0", "back1"), ("up0", "up1"))
-        turn_weights(2, 4, "turn0")
+        turn_weights(2, 4, "gate0")
         for seg in range(1, S // SEG):
             lo, hi = seg * SEG, (seg + 1) * SEG
             if seg == 2:

@@ -51,7 +51,7 @@ def tile_list_tabhs_g_none_kernel(tc, tab, w4_words, w4_scales, w8, wgo, offs, o
         w4_plane = keep.tile([P, M // 4], I32, name="w4_plane", align_bytes=64)
         nc.vector.memset(w4_plane[:], 0)
 
-        warm = keep.tile([P, 16], F32, name="warm")
+        warm = keep.tile([P, 16], F32, name="warm", tag="warm", align_bytes=64)
         nc.vector.memset(warm[:, :8], 0.0)
         nc.scalar.activation(warm[:, 8:9], warm[:, 0:1], SILU)
 
@@ -71,8 +71,10 @@ def tile_list_tabhs_g_none_kernel(tc, tab, w4_words, w4_scales, w8, wgo, offs, o
         def scales_of(lo, hi):
             return got_planes[lo // HALF][:].bitcast(U8)[:, lo % HALF : lo % HALF + hi - lo]
 
-        zeros = keep.tile([P, P], F32, name="zeros", tag="early", align_bytes=64)
+        zeros = keep.tile([P, P], F32, name="zeros", align_bytes=64)
         nc.vector.memset(zeros[:], 0.0)
+        window0 = keep.tile([P, T], F32, name="window0", align_bytes=64)
+        nc.vector.memset(window0[:], 0.0)
         ident = keep.tile([P, P], F32, name="ident")
         nc.gpsimd.affine_select(
             out=ident[:],
@@ -102,7 +104,7 @@ def tile_list_tabhs_g_none_kernel(tc, tab, w4_words, w4_scales, w8, wgo, offs, o
             if lo == 0:
                 nc.sync.dma_start(place[:], offs2)
 
-        w8_bf = keep.tile([P, M, PACK], BF16, name="w8_bf", tag="late", align_bytes=64)
+        w8_bf = keep.tile([P, M, PACK], BF16, name="w8_bf", align_bytes=64)
         nc.scalar.copy(
             w8_bf[:].rearrange("p (c j) i -> p c i j", j=PACK), w8_raw[:].rearrange("p i (c j) -> p c i j", j=PACK)
         )
@@ -116,9 +118,7 @@ def tile_list_tabhs_g_none_kernel(tc, tab, w4_words, w4_scales, w8, wgo, offs, o
                 got_words[:, lo:hi], tab_words[:].bitcast(U32).indirect(pick[:, lo // STRIPE : hi // STRIPE])
             )
 
-        window0 = keep.tile([P, T], F32, name="window0", tag="late", align_bytes=64)
-        nc.gpsimd.memset(window0[:], 0.0)
-        window1 = keep.tile([P, T], F32, name="window1", tag="early", align_bytes=64)
+        window1 = keep.tile([P, T], F32, name="window1", tag="warm", align_bytes=64)
         nc.gpsimd.memset(window1[:], 0.0)
         windows = [window0, window1]
 
@@ -133,9 +133,9 @@ def tile_list_tabhs_g_none_kernel(tc, tab, w4_words, w4_scales, w8, wgo, offs, o
                 stop=True,
             )
 
-        def gate_pass(dst, m, lo):
+        def gate_pass(dst, m, lo, width=SEG):
             codes = w4_codes[:].bitcast(U8)[:, 2 * P * m : 2 * P * (m + 1)].bitcast(FP4X4)
-            project(dst, codes, w4_plane[:].bitcast(U8)[:, P * m : P * (m + 1)], lo, lo + SEG)
+            project(dst, codes, w4_plane[:].bitcast(U8)[:, P * m : P * (m + 1)], lo, lo + width)
 
         gated = keep.tile([P, 2, S], F32, name="gated")
         weighted = keep.tile([P, 2, S], F32, name="weighted")
@@ -148,13 +148,27 @@ def tile_list_tabhs_g_none_kernel(tc, tab, w4_words, w4_scales, w8, wgo, offs, o
                 MULT,
             )
 
-        for m in range(2):
+        def first_up(m):
             up = psum.tile([P, SEG], F32, name="up%d" % m, tag="up%d" % m)
             project(up[:], w8_codes[:, P * m : P * (m + 1)].bitcast(FP8X4), w8_plane[:, P * m : P * (m + 1)], 0, SEG)
-            nc.vector.tensor_tensor(weighted[:, m, :SEG], up[:], weights[:, :SEG], MULT)
+            return up
+
+        def first_gate(m, dst):
             gate = psum.tile([P, SEG], F32, name="gate%d" % m, tag="gate%d" % m)
             gate_pass(gate[:], m, 0)
-            nc.scalar.activation(gated[:, m, :SEG], gate[:], SILU)
+            nc.scalar.activation(dst, gate[:], SILU)
+
+        first_silu = keep.tile([P, SEG], F32, name="first_silu")
+        for lo, tag in ((0, "back0"), (P, "gate0")):
+            gate = psum.tile([P, P], F32, name="first_gate%d" % lo, tag=tag)
+            gate_pass(gate[:], 0, lo, P)
+            nc.scalar.activation(first_silu[:, lo : lo + P], gate[:], SILU)
+            nc.gpsimd.tensor_tensor(
+                weighted[:, 0, lo : lo + P], first_silu[:, lo : lo + P], weights[:, lo : lo + P], MULT
+            )
+        nc.scalar.copy(gated[:, 0, :SEG], first_up(0)[:])
+        nc.vector.tensor_tensor(weighted[:, 1, :SEG], first_up(1)[:], weights[:, :SEG], MULT)
+        first_gate(1, gated[:, 1, :SEG])
         for m in range(2):
             scatter(m, 0, SEG)
 

@@ -49,11 +49,11 @@ def tile_list_tabhs_g_none_kernel(tc, tab, w4_words, w4_scales, w8, wgo, offs, o
         nc.sync.dma_start(pick[:], offs)
 
         w4_plane = keep.tile([P, M // 4], I32, name="w4_plane", align_bytes=64)
-        nc.vector.memset(w4_plane[:], 0)
 
-        warm = keep.tile([P, 16], F32, name="warm", tag="warm", align_bytes=64)
-        nc.vector.memset(warm[:, :8], 0.0)
-        nc.scalar.activation(warm[:, 8:9], warm[:, 0:1], SILU)
+        zeros = keep.tile([P, P], F32, name="zeros", tag="zeros", align_bytes=64)
+        nc.vector.memset(zeros[:], 0.0)
+        warm = keep.tile([P, 1], F32, name="warm")
+        nc.scalar.activation(warm[:], zeros[:, 0:1], SILU)
 
         nc.sync.dma_start(out=w8_raw[:, 1:, :], in_=w8_rows[:, 1:, :])
         w4_rows = [w4_scales[0].bitcast(I32)[r:16:4, :] for r in range(4)]
@@ -65,14 +65,10 @@ def tile_list_tabhs_g_none_kernel(tc, tab, w4_words, w4_scales, w8, wgo, offs, o
         load_scale_rows(nc.sync, w4_plane, w4_rows, (3,))
 
         got_planes = [keep.tile([P, HALF // 4], I32, name="got_plane%d" % h, align_bytes=64) for h in range(2)]
-        for plane in got_planes:
-            nc.vector.memset(plane[:], 0)
 
         def scales_of(lo, hi):
             return got_planes[lo // HALF][:].bitcast(U8)[:, lo % HALF : lo % HALF + hi - lo]
 
-        zeros = keep.tile([P, P], F32, name="zeros", align_bytes=64)
-        nc.vector.memset(zeros[:], 0.0)
         window0 = keep.tile([P, T], F32, name="window0", align_bytes=64)
         nc.vector.memset(window0[:], 0.0)
         ident = keep.tile([P, P], F32, name="ident")
@@ -91,7 +87,8 @@ def tile_list_tabhs_g_none_kernel(tc, tab, w4_words, w4_scales, w8, wgo, offs, o
         place = keep.tile([P, S // STRIPE], U16, name="place")
 
         for lo, hi in ((0, S // 2), (S // 2, S)):
-            nc.sync.dma_start(out=weights[:, lo:hi], in_=wgo[:, lo:hi])
+            cols = slice(0, SEG) if lo == 0 else slice(SEG, S)
+            nc.sync.dma_start(out=weights[:, cols], in_=wgo[:, cols])
             got_scales = keep.tile([P, HALF], U8, name="got_scales%d" % lo, align_bytes=64)
             nc.vector.tensor_copy(
                 got_scales[:], tab_scales[:].bitcast(U8).indirect(pick[:, lo // STRIPE : hi // STRIPE])
@@ -118,7 +115,7 @@ def tile_list_tabhs_g_none_kernel(tc, tab, w4_words, w4_scales, w8, wgo, offs, o
                 got_words[:, lo:hi], tab_words[:].bitcast(U32).indirect(pick[:, lo // STRIPE : hi // STRIPE])
             )
 
-        window1 = keep.tile([P, T], F32, name="window1", tag="warm", align_bytes=64)
+        window1 = keep.tile([P, T], F32, name="window1", tag="zeros", align_bytes=64)
         nc.gpsimd.memset(window1[:], 0.0)
         windows = [window0, window1]
 

@@ -40,6 +40,10 @@ def tile_list_tabhs_g_none_kernel(tc, tab, w4_words, w4_scales, w8, wgo, offs, o
         w8_raw = keep.tile([P, PACK, M], F32, name="w8_raw", tag="raw", align_bytes=64)
         w8_rows = w8.rearrange("(p i) n -> p i n", i=PACK)
 
+        warm = keep.tile([P, 16], F32, name="warm")
+        nc.vector.memset(warm[:, :8], 0.0)
+        nc.scalar.activation(warm[:, 8:9], warm[:, 0:1], SILU)
+
         nc.sync.dma_start(out=w8_raw[:, :1, :], in_=w8_rows[:, :1, :])
         tab_scales = keep.tile([P, T // 4], I32, name="tab_scales", align_bytes=64)
         nc.vector.memset(tab_scales[: P - 16, :], 0)
@@ -52,8 +56,6 @@ def tile_list_tabhs_g_none_kernel(tc, tab, w4_words, w4_scales, w8, wgo, offs, o
 
         zeros = keep.tile([P, P], F32, name="zeros", tag="zeros", align_bytes=64)
         nc.vector.memset(zeros[:], 0.0)
-        warm = keep.tile([P, 1], F32, name="warm")
-        nc.scalar.activation(warm[:], zeros[:, 0:1], SILU)
 
         nc.sync.dma_start(out=w8_raw[:, 1:, :], in_=w8_rows[:, 1:, :])
         w4_rows = [w4_scales[0].bitcast(I32)[r:16:4, :] for r in range(4)]

@@ -103,13 +103,19 @@ def tile_list_tabhs_g_none_kernel(tc, tab, w4_words, w4_scales, w8, wgo, offs, o
             if lo == 0:
                 nc.sync.dma_start(place[:], offs2)
 
-        w8_bf = keep.tile([P, M, PACK], BF16, name="w8_bf", align_bytes=64)
-        nc.scalar.copy(
-            w8_bf[:].rearrange("p (c j) i -> p c i j", j=PACK), w8_raw[:].rearrange("p i (c j) -> p c i j", j=PACK)
-        )
         w8_codes = keep.tile([P, M], U32, name="w8_codes", align_bytes=64)
         w8_plane = keep.tile([P, M], U8, name="w8_plane", align_bytes=64)
-        nc.vector.quantize_mx(out=w8_codes[:].bitcast(FP8X4), scales=w8_plane[:], in_=w8_bf[:].rearrange("p n i -> p (n i)"))
+        for m in range(2):
+            w8_bf = keep.tile([P, P, PACK], BF16, name="w8_bf%d" % m, align_bytes=64)
+            nc.scalar.copy(
+                w8_bf[:].rearrange("p (c j) i -> p c i j", j=PACK),
+                w8_raw[:, :, P * m : P * (m + 1)].rearrange("p i (c j) -> p c i j", j=PACK),
+            )
+            nc.vector.quantize_mx(
+                out=w8_codes[:, P * m : P * (m + 1)].bitcast(FP8X4),
+                scales=w8_plane[:, P * m : P * (m + 1)],
+                in_=w8_bf[:].rearrange("p n i -> p (n i)"),
+            )
 
         got_words = keep.tile([P, S], U32, name="got_words", tag="raw", align_bytes=64)
         for lo, hi in ((0, SEG), (SEG, 2 * SEG), (2 * SEG, S)):

@@ -21,13 +21,20 @@ P = 128
 PACK = 4
 STRIPE = 16
 GROUPS = 8
-SEG = 256
-LAST = 384
+UNITS = S // P
 HALF = S // 2
+WORD_CUTS = (0, 256, 512, S)
+SCATTERS = (
+    (0, 0, 128), (1, 0, 128), (0, 128, 256), (1, 128, 256), (0, 256, 384), (1, 256, 384), (0, 384, 512), (1, 384, 512),
+    (0, 512, 768), (1, 512, 672), (0, 768, S), (1, 672, S),
+)
+UP_BANKS = {1: "b2", 2: "b0", 3: "b7", 4: "b2", 5: "b6", 6: "b5", 7: "b0"}
+GATE_BANKS = {1: "b1", 2: "b6", 3: "b5", 4: "b0", 5: "b7", 6: "b2", 7: "b6"}
+BACK_BANKS = {2: "b1", 3: "b3", 4: "b4", 5: "b1", 6: "b3", 7: "b4"}
 
 
-def load_scale_rows(queue, plane, rows, which=range(4)):
-    for r in which:
+def load_scale_rows(queue, plane, rows):
+    for r in range(4):
         queue.dma_start(out=plane[r:P:32, :], in_=rows[r])
 
 
@@ -44,7 +51,6 @@ def tile_list_tabhs_g_none_kernel(tc, tab, w4_words, w4_scales, w8, wgo, offs, o
         nc.vector.memset(warm[:, :8], 0.0)
         nc.scalar.activation(warm[:, 8:9], warm[:, 0:1], SILU)
 
-        nc.sync.dma_start(out=w8_raw[:, :1, :], in_=w8_rows[:, :1, :])
         tab_scales = keep.tile([P, T // 4], I32, name="tab_scales", align_bytes=64)
         nc.vector.memset(tab_scales[: P - 16, :], 0)
         nc.sync.dma_start(out=tab_scales[P - 16 :, :], in_=tab[0, K * T :].bitcast(I32).rearrange("(q t) -> q t", q=16))
@@ -57,19 +63,22 @@ def tile_list_tabhs_g_none_kernel(tc, tab, w4_words, w4_scales, w8, wgo, offs, o
         zeros = keep.tile([P, P], F32, name="zeros", tag="zeros", align_bytes=64)
         nc.vector.memset(zeros[:], 0.0)
 
-        nc.sync.dma_start(out=w8_raw[:, 1:, :], in_=w8_rows[:, 1:, :])
+        nc.sync.dma_start(out=w8_raw[:], in_=w8_rows)
         w4_rows = [w4_scales[0].bitcast(I32)[r:16:4, :] for r in range(4)]
-        load_scale_rows(nc.sync, w4_plane, w4_rows, (0, 1, 2))
+        load_scale_rows(nc.sync, w4_plane, w4_rows)
         tab_words = keep.tile([P, T], I32, name="tab_words", align_bytes=64)
         nc.sync.dma_start(out=tab_words[:], in_=tab[0, : K * T].bitcast(I32).rearrange("(p t) -> p t", p=P))
         w4_codes = keep.tile([P, M // 2], I32, name="w4_codes", align_bytes=64)
         nc.sync.dma_start(out=w4_codes[:], in_=w4_words[0].bitcast(I32))
-        load_scale_rows(nc.sync, w4_plane, w4_rows, (3,))
+        group_rows = keep.tile([P, P], F32, name="group_rows")
+        nc.vector.memset(group_rows[GROUPS * UNITS :, :], 0.0)
+        nc.sync.dma_start(
+            out=group_rows[: GROUPS * UNITS, :], in_=wgo[0:P:STRIPE, :].rearrange("g (c j) -> g c j", j=P)
+        )
+        weights = keep.tile([P, P], F32, name="weights", align_bytes=64)
+        nc.sync.dma_start(out=weights[:], in_=wgo[:, :P])
 
         got_planes = [keep.tile([P, HALF // 4], I32, name="got_plane%d" % h, align_bytes=64) for h in range(2)]
-
-        def scales_of(lo, hi):
-            return got_planes[lo // HALF][:].bitcast(U8)[:, lo % HALF : lo % HALF + hi - lo]
 
         window0 = keep.tile([P, T], F32, name="window0", align_bytes=64)
         nc.vector.memset(window0[:], 0.0)
@@ -84,13 +93,9 @@ def tile_list_tabhs_g_none_kernel(tc, tab, w4_words, w4_scales, w8, wgo, offs, o
             channel_multiplier=1,
         )
 
-
-        weights = keep.tile([P, S], F32, name="weights", align_bytes=64)
         place = keep.tile([P, S // STRIPE], U16, name="place")
 
-        for lo, hi in ((0, S // 2), (S // 2, S)):
-            cols = slice(0, SEG) if lo == 0 else slice(SEG, S)
-            nc.sync.dma_start(out=weights[:, cols], in_=wgo[:, cols])
+        for lo, hi in ((0, HALF), (HALF, S)):
             got_scales = keep.tile([P, HALF], U8, name="got_scales%d" % lo, align_bytes=64)
             nc.vector.tensor_copy(
                 got_scales[:], tab_scales[:].bitcast(U8).indirect(pick[:, lo // STRIPE : hi // STRIPE])
@@ -118,7 +123,7 @@ def tile_list_tabhs_g_none_kernel(tc, tab, w4_words, w4_scales, w8, wgo, offs, o
             )
 
         got_words = keep.tile([P, S], U32, name="got_words", tag="raw", align_bytes=64)
-        for lo, hi in ((0, SEG), (SEG, 2 * SEG), (2 * SEG, S)):
+        for lo, hi in zip(WORD_CUTS, WORD_CUTS[1:]):
             nc.vector.tensor_copy(
                 got_words[:, lo:hi], tab_words[:].bitcast(U32).indirect(pick[:, lo // STRIPE : hi // STRIPE])
             )
@@ -127,107 +132,118 @@ def tile_list_tabhs_g_none_kernel(tc, tab, w4_words, w4_scales, w8, wgo, offs, o
         nc.gpsimd.memset(window1[:], 0.0)
         windows = [window0, window1]
 
-        def project(dst, codes, plane, lo, hi):
+        def table_codes(unit, units=1):
+            return got_words[:, P * unit : P * (unit + units)].bitcast(FP8X4)
+
+        def table_plane(unit, units=1):
+            at = P * unit % HALF
+            return got_planes[P * unit // HALF][:].bitcast(U8)[:, at : at + P * units]
+
+        def gate_pass(dst, m, unit, units=1):
             nc.tensor.matmul_mx(
                 out=dst,
-                lhsT=codes,
-                lhsT_scale=plane,
-                rhs=got_words[:, lo:hi].bitcast(FP8X4),
-                rhs_scale=scales_of(lo, hi),
+                lhsT=w4_codes[:].bitcast(U8)[:, 2 * P * m : 2 * P * (m + 1)].bitcast(FP4X4),
+                lhsT_scale=w4_plane[:].bitcast(U8)[:, P * m : P * (m + 1)],
+                rhs=table_codes(unit, units),
+                rhs_scale=table_plane(unit, units),
                 start=True,
                 stop=True,
             )
 
-        def gate_pass(dst, m, lo, width=SEG):
-            codes = w4_codes[:].bitcast(U8)[:, 2 * P * m : 2 * P * (m + 1)].bitcast(FP4X4)
-            project(dst, codes, w4_plane[:].bitcast(U8)[:, P * m : P * (m + 1)], lo, lo + width)
-
-        gated = keep.tile([P, 2, S], F32, name="gated")
-        weighted = keep.tile([P, 2, S], F32, name="weighted")
-
-        def scatter(m, lo, hi):
-            nc.vector.tensor_tensor(
-                windows[m][:].indirect(place[:, lo // STRIPE : hi // STRIPE]),
-                gated[:, m, lo:hi],
-                weighted[:, m, lo:hi],
-                MULT,
+        def first_up(m, tag):
+            up = psum.tile([P, P], F32, name="up%d" % m, tag=tag)
+            nc.tensor.matmul_mx(
+                out=up[:],
+                lhsT=w8_codes[:, P * m : P * (m + 1)].bitcast(FP8X4),
+                lhsT_scale=w8_plane[:, P * m : P * (m + 1)],
+                rhs=table_codes(0),
+                rhs_scale=table_plane(0),
+                start=True,
+                stop=True,
             )
-
-        def first_up(m):
-            up = psum.tile([P, SEG], F32, name="up%d" % m, tag="up%d" % m)
-            project(up[:], w8_codes[:, P * m : P * (m + 1)].bitcast(FP8X4), w8_plane[:, P * m : P * (m + 1)], 0, SEG)
             return up
 
-        def first_gate(m, dst):
-            gate = psum.tile([P, SEG], F32, name="gate%d" % m, tag="gate%d" % m)
+        left = keep.tile([P, 2, S], F32, name="left")
+        right = keep.tile([P, 2, S], F32, name="right")
+        token_weights = keep.tile([P, GROUPS, UNITS], F32, name="token_weights")
+        turned = psum.tile([P, P], F32, name="turned", tag="b0")
+        nc.tensor.transpose(turned[:], group_rows[:], ident[:])
+        nc.scalar.copy(token_weights[:].rearrange("p g c -> p (g c)"), turned[:, : GROUPS * UNITS])
+
+        def first_gate(m, tag):
+            gate = psum.tile([P, P], F32, name="first_gate%d" % m, tag=tag)
             gate_pass(gate[:], m, 0)
-            nc.scalar.activation(dst, gate[:], SILU)
+            silu = keep.tile([P, P], F32, name="first_silu%d" % m, tag="first_silu")
+            nc.scalar.activation(silu[:], gate[:], SILU)
+            return silu
 
-        first_silu = keep.tile([P, SEG], F32, name="first_silu")
-        for lo, tag in ((0, "back0"), (P, "gate0")):
-            gate = psum.tile([P, P], F32, name="first_gate%d" % lo, tag=tag)
-            gate_pass(gate[:], 0, lo, P)
-            nc.scalar.activation(first_silu[:, lo : lo + P], gate[:], SILU)
-            nc.gpsimd.tensor_tensor(
-                weighted[:, 0, lo : lo + P], first_silu[:, lo : lo + P], weights[:, lo : lo + P], MULT
+        def turned_up(unit):
+            up_t = psum.tile([P, M], F32, name="up_t%d" % unit, tag=UP_BANKS[unit])
+            nc.tensor.matmul_mx(
+                out=up_t[:],
+                lhsT=table_codes(unit),
+                lhsT_scale=table_plane(unit),
+                rhs=w8_codes[:].bitcast(FP8X4),
+                rhs_scale=w8_plane[:],
+                start=True,
+                stop=True,
             )
-        nc.scalar.copy(gated[:, 0, :SEG], first_up(0)[:])
-        nc.vector.tensor_tensor(weighted[:, 1, :SEG], first_up(1)[:], weights[:, :SEG], MULT)
-        first_gate(1, gated[:, 1, :SEG])
-        for m in range(2):
-            scatter(m, 0, SEG)
+            return up_t
 
-        token_weights = keep.tile([P, S // P, GROUPS], F32, name="token_weights")
-
-        def turn_weights(first, last, tag):
-            turned = psum.tile([P, last - first, P], F32, name="turned%d" % first, tag=tag)
-            for c in range(first, last):
-                nc.tensor.transpose(turned[:, c - first, :], weights[:, P * c : P * (c + 1)], ident[:])
-            nc.scalar.copy(
-                token_weights[:, first:last, :], turned[:].rearrange("p c (g s) -> p c g s", s=STRIPE)[:, :, :, 0]
-            )
-
-        up_tags = ("turn0", "gate1", "turn0")
-        gate_tags = ("gate0", "turn1", "gate0")
-        back_tags = (("up0", "up1"), ("back0", "back1"), ("up0", "up1"))
-        turn_weights(2, 4, "gate0")
-        for seg in range(1, S // SEG):
-            lo, hi = seg * SEG, (seg + 1) * SEG
-            if seg == 2:
-                turn_weights(4, 8, "turn1")
-            up_t = psum.tile([P, 2, M], F32, name="up_t%d" % seg, tag=up_tags[seg - 1])
-            scaled = keep.tile([P, 2, 2, GROUPS, STRIPE], F32, name="scaled%d" % seg)
-            for i in range(2):
-                at = lo + P * i
-                nc.tensor.matmul_mx(
-                    out=up_t[:, i, :],
-                    lhsT=got_words[:, at : at + P].bitcast(FP8X4),
-                    lhsT_scale=scales_of(at, at + P),
-                    rhs=w8_codes[:].bitcast(FP8X4),
-                    rhs_scale=w8_plane[:],
-                    start=True,
-                    stop=True,
+        def weigh(unit, up_t):
+            scaled = keep.tile([P, 2, GROUPS, STRIPE], F32, name="scaled%d" % unit, tag="scaled%d" % max(unit, 2))
+            for g in range(GROUPS):
+                nc.scalar.activation(
+                    scaled[:, :, g, :],
+                    up_t[:].rearrange("p (m g s) -> p m g s", g=GROUPS, s=STRIPE)[:, :, g, :],
+                    COPY,
+                    scale=token_weights[:, g, unit : unit + 1],
                 )
-            for i in range(2):
-                for g in range(GROUPS):
-                    nc.scalar.activation(
-                        scaled[:, i, :, g, :],
-                        up_t[:, i, :].rearrange("p (m g s) -> p m g s", g=GROUPS, s=STRIPE)[:, :, g, :],
-                        COPY,
-                        scale=token_weights[:, 2 * seg + i, g : g + 1],
+            return scaled
+
+        def gate_unit(unit):
+            gates = psum.tile([P, 2, P], F32, name="gates%d" % unit, tag=GATE_BANKS[unit])
+            for m in range(2):
+                gate_pass(gates[:, m, :], m, unit)
+            nc.scalar.activation(left[:, :, P * unit : P * (unit + 1)], gates[:], SILU)
+
+        def turn_back(unit, scaled, tiles, tag):
+            back = psum.tile([P, len(tiles), P], F32, name="back%d_%d" % (unit, tiles[0]), tag=tag)
+            for at, m in enumerate(tiles):
+                nc.tensor.transpose(back[:, at, :], scaled[:, m].rearrange("p g s -> p (g s)"), ident[:])
+            nc.scalar.copy(right[:, tiles[0] : tiles[-1] + 1, P * unit : P * (unit + 1)], back[:])
+
+        lefts = {}
+
+        def scatter_through(unit):
+            for m, lo, hi in SCATTERS:
+                if (hi - 1) // P == unit:
+                    nc.vector.tensor_tensor(
+                        windows[m][:].indirect(place[:, lo // STRIPE : hi // STRIPE]),
+                        lefts.get((m, lo), left[:, m, lo:hi]),
+                        right[:, m, lo:hi],
+                        MULT,
                     )
-            gates = psum.tile([P, 2, SEG], F32, name="gates%d" % seg, tag=gate_tags[seg - 1])
-            for m in range(2):
-                gate_pass(gates[:, m, :], m, lo)
-            nc.scalar.activation(gated[:, :, lo:hi], gates[:], SILU)
-            for m in range(2):
-                back = psum.tile([P, 2, P], F32, name="back%d_%d" % (seg, m), tag=back_tags[seg - 1][m])
-                for i in range(2):
-                    nc.tensor.transpose(back[:, i, :], scaled[:, i, m].rearrange("p g s -> p (g s)"), ident[:])
-                nc.scalar.copy(weighted[:, m, lo:hi], back[:].rearrange("p i j -> p (i j)"))
-            scatter(0, lo, hi)
-            if seg < 3:
-                scatter(1, lo, min(hi, S - LAST))
-        nc.sync.dma_start(out=out[:P, :], in_=window0[:])
-        scatter(1, S - LAST, S)
-        nc.sync.dma_start(out=out[P:, :], in_=window1[:])
+                    if hi == S:
+                        nc.sync.dma_start(out=out[P * m : P * (m + 1), :], in_=windows[m][:])
+
+        nc.gpsimd.tensor_tensor(right[:, 0, :P], first_gate(0, "b1")[:], weights[:], MULT)
+        second_up = turned_up(1)
+        nc.scalar.copy(left[:, 0, :P], first_up(0, "b3")[:])
+        nc.vector.tensor_tensor(right[:, 1, :P], first_up(1, "b4")[:], weights[:], MULT)
+        scaled = weigh(1, second_up)
+        lefts[1, 0] = first_gate(1, "b5")[:]
+        scatter_through(0)
+        gate_unit(1)
+        turn_back(1, scaled, (0,), "b6")
+        turn_back(1, scaled, (1,), "b7")
+        scatter_through(1)
+        for unit in range(2, UNITS):
+            scaled = weigh(unit, turned_up(unit))
+            gate_unit(unit)
+            if unit == 2:
+                turn_back(unit, scaled, (0,), "b1")
+                turn_back(unit, scaled, (1,), "b3")
+            else:
+                turn_back(unit, scaled, (0, 1), BACK_BANKS[unit])
+            scatter_through(unit)

from contextlib import ExitStack

import concourse.mybir as mybir

K, M, T, S = 512, 256, 2048, 1024
FLOPS = 2 * 2 * K * M * S

F32 = mybir.dt.float32
BF16 = mybir.dt.bfloat16
I32 = mybir.dt.int32
U32 = mybir.dt.uint32
U16 = mybir.dt.uint16
U8 = mybir.dt.uint8
FP8X4 = mybir.dt.float8_e4m3fn_x4
FP4X4 = mybir.dt.float4_e2m1fn_x4
MULT = mybir.AluOpType.mult
SILU = mybir.ActivationFunctionType.Silu
COPY = mybir.ActivationFunctionType.Copy

P = 128
PACK = 4
STRIPE = 16
GROUPS = 8
UNITS = S // P
HALF = S // 2
WORD_CUTS = (0, 256, 512, S)
SCATTERS = (
    (0, 0, 128), (1, 0, 128), (0, 128, 256), (1, 128, 256), (0, 256, 384), (1, 256, 384), (0, 384, 512), (1, 384, 512),
    (0, 512, 768), (1, 512, 672), (0, 768, S), (1, 672, S),
)
UP_BANKS = {1: "b2", 2: "b0", 3: "b7", 4: "b2", 5: "b6", 6: "b5", 7: "b0"}
GATE_BANKS = {1: "b1", 2: "b6", 3: "b5", 4: "b0", 5: "b7", 6: "b2", 7: "b6"}
BACK_BANKS = {2: "b1", 3: "b3", 4: "b4", 5: "b1", 6: "b3", 7: "b4"}


def load_scale_rows(queue, plane, rows):
    for r in range(4):
        queue.dma_start(out=plane[r:P:32, :], in_=rows[r])


def tile_list_tabhs_g_none_kernel(tc, tab, w4_words, w4_scales, w8, wgo, offs, offs2, out):
    nc = tc.nc
    with ExitStack() as ctx:
        keep = ctx.enter_context(tc.tile_pool(name="keep", bufs=1))
        psum = ctx.enter_context(tc.psum_pool(name="psum", bufs=1))

        w8_raw = keep.tile([P, PACK, M], F32, name="w8_raw", tag="raw", align_bytes=64)
        w8_rows = w8.rearrange("(p i) n -> p i n", i=PACK)

        warm = keep.tile([P, 16], F32, name="warm")
        nc.vector.memset(warm[:, :8], 0.0)
        nc.scalar.activation(warm[:, 8:9], warm[:, 0:1], SILU)

        tab_scales = keep.tile([P, T // 4], I32, name="tab_scales", align_bytes=64)
        nc.vector.memset(tab_scales[: P - 16, :], 0)
        nc.sync.dma_start(out=tab_scales[P - 16 :, :], in_=tab[0, K * T :].bitcast(I32).rearrange("(q t) -> q t", q=16))

        pick = keep.tile([P, S // STRIPE], U16, name="pick")
        nc.sync.dma_start(pick[:], offs)

        w4_plane = keep.tile([P, M // 4], I32, name="w4_plane", align_bytes=64)

        zeros = keep.tile([P, P], F32, name="zeros", tag="zeros", align_bytes=64)
        nc.vector.memset(zeros[:], 0.0)

        nc.sync.dma_start(out=w8_raw[:], in_=w8_rows)
        w4_rows = [w4_scales[0].bitcast(I32)[r:16:4, :] for r in range(4)]
        load_scale_rows(nc.sync, w4_plane, w4_rows)
        tab_words = keep.tile([P, T], I32, name="tab_words", align_bytes=64)
        nc.sync.dma_start(out=tab_words[:], in_=tab[0, : K * T].bitcast(I32).rearrange("(p t) -> p t", p=P))
        w4_codes = keep.tile([P, M // 2], I32, name="w4_codes", align_bytes=64)
        nc.sync.dma_start(out=w4_codes[:], in_=w4_words[0].bitcast(I32))
        group_rows = keep.tile([P, P], F32, name="group_rows")
        nc.vector.memset(group_rows[GROUPS * UNITS :, :], 0.0)
        nc.sync.dma_start(
            out=group_rows[: GROUPS * UNITS, :], in_=wgo[0:P:STRIPE, :].rearrange("g (c j) -> g c j", j=P)
        )
        weights = keep.tile([P, P], F32, name="weights", align_bytes=64)
        nc.sync.dma_start(out=weights[:], in_=wgo[:, :P])

        got_planes = [keep.tile([P, HALF // 4], I32, name="got_plane%d" % h, align_bytes=64) for h in range(2)]

        window0 = keep.tile([P, T], F32, name="window0", align_bytes=64)
        nc.vector.memset(window0[:], 0.0)
        ident = keep.tile([P, P], F32, name="ident")
        nc.gpsimd.affine_select(
            out=ident[:],
            in_=zeros[:],
            compare_op=mybir.AluOpType.not_equal,
            fill=1.0,
            base=0,
            pattern=[[-1, P]],
            channel_multiplier=1,
        )

        place = keep.tile([P, S // STRIPE], U16, name="place")

        for lo, hi in ((0, HALF), (HALF, S)):
            got_scales = keep.tile([P, HALF], U8, name="got_scales%d" % lo, align_bytes=64)
            nc.vector.tensor_copy(
                got_scales[:], tab_scales[:].bitcast(U8).indirect(pick[:, lo // STRIPE : hi // STRIPE])
            )
            load_scale_rows(
                nc.sync,
                got_planes[lo // HALF],
                [got_scales[P - 16 + r : P : 4, :].bitcast(I32) for r in range(4)],
            )
            if lo == 0:
                nc.sync.dma_start(place[:], offs2)

        w8_codes = keep.tile([P, M], U32, name="w8_codes", align_bytes=64)
        w8_plane = keep.tile([P, M], U8, name="w8_plane", align_bytes=64)
        for m in range(2):
            w8_bf = keep.tile([P, P, PACK], BF16, name="w8_bf%d" % m, align_bytes=64)
            nc.scalar.copy(
                w8_bf[:].rearrange("p (c j) i -> p c i j", j=PACK),
                w8_raw[:, :, P * m : P * (m + 1)].rearrange("p i (c j) -> p c i j", j=PACK),
            )
            nc.vector.quantize_mx(
                out=w8_codes[:, P * m : P * (m + 1)].bitcast(FP8X4),
                scales=w8_plane[:, P * m : P * (m + 1)],
                in_=w8_bf[:].rearrange("p n i -> p (n i)"),
            )

        got_words = keep.tile([P, S], U32, name="got_words", tag="raw", align_bytes=64)
        for lo, hi in zip(WORD_CUTS, WORD_CUTS[1:]):
            nc.vector.tensor_copy(
                got_words[:, lo:hi], tab_words[:].bitcast(U32).indirect(pick[:, lo // STRIPE : hi // STRIPE])
            )

        window1 = keep.tile([P, T], F32, name="window1", tag="zeros", align_bytes=64)
        nc.gpsimd.memset(window1[:], 0.0)
        windows = [window0, window1]

        def table_codes(unit, units=1):
            return got_words[:, P * unit : P * (unit + units)].bitcast(FP8X4)

        def table_plane(unit, units=1):
            at = P * unit % HALF
            return got_planes[P * unit // HALF][:].bitcast(U8)[:, at : at + P * units]

        def gate_pass(dst, m, unit, units=1):
            nc.tensor.matmul_mx(
                out=dst,
                lhsT=w4_codes[:].bitcast(U8)[:, 2 * P * m : 2 * P * (m + 1)].bitcast(FP4X4),
                lhsT_scale=w4_plane[:].bitcast(U8)[:, P * m : P * (m + 1)],
                rhs=table_codes(unit, units),
                rhs_scale=table_plane(unit, units),
                start=True,
                stop=True,
            )

        def first_up(m, tag):
            up = psum.tile([P, P], F32, name="up%d" % m, tag=tag)
            nc.tensor.matmul_mx(
                out=up[:],
                lhsT=w8_codes[:, P * m : P * (m + 1)].bitcast(FP8X4),
                lhsT_scale=w8_plane[:, P * m : P * (m + 1)],
                rhs=table_codes(0),
                rhs_scale=table_plane(0),
                start=True,
                stop=True,
            )
            return up

        left = keep.tile([P, 2, S], F32, name="left")
        right = keep.tile([P, 2, S], F32, name="right")
        token_weights = keep.tile([P, GROUPS, UNITS], F32, name="token_weights")
        turned = psum.tile([P, P], F32, name="turned", tag="b0")
        nc.tensor.transpose(turned[:], group_rows[:], ident[:])
        nc.scalar.copy(token_weights[:].rearrange("p g c -> p (g c)"), turned[:, : GROUPS * UNITS])

        def first_gate(m, tag):
            gate = psum.tile([P, P], F32, name="first_gate%d" % m, tag=tag)
            gate_pass(gate[:], m, 0)
            silu = keep.tile([P, P], F32, name="first_silu%d" % m, tag="first_silu")
            nc.scalar.activation(silu[:], gate[:], SILU)
            return silu

        def turned_up(unit):
            up_t = psum.tile([P, M], F32, name="up_t%d" % unit, tag=UP_BANKS[unit])
            nc.tensor.matmul_mx(
                out=up_t[:],
                lhsT=table_codes(unit),
                lhsT_scale=table_plane(unit),
                rhs=w8_codes[:].bitcast(FP8X4),
                rhs_scale=w8_plane[:],
                start=True,
                stop=True,
            )
            return up_t

        def weigh(unit, up_t):
            scaled = keep.tile([P, 2, GROUPS, STRIPE], F32, name="scaled%d" % unit, tag="scaled%d" % max(unit, 2))
            for g in range(GROUPS):
                nc.scalar.activation(
                    scaled[:, :, g, :],
                    up_t[:].rearrange("p (m g s) -> p m g s", g=GROUPS, s=STRIPE)[:, :, g, :],
                    COPY,
                    scale=token_weights[:, g, unit : unit + 1],
                )
            return scaled

        def gate_unit(unit):
            gates = psum.tile([P, 2, P], F32, name="gates%d" % unit, tag=GATE_BANKS[unit])
            for m in range(2):
                gate_pass(gates[:, m, :], m, unit)
            nc.scalar.activation(left[:, :, P * unit : P * (unit + 1)], gates[:], SILU)

        def turn_back(unit, scaled, tiles, tag):
            back = psum.tile([P, len(tiles), P], F32, name="back%d_%d" % (unit, tiles[0]), tag=tag)
            for at, m in enumerate(tiles):
                nc.tensor.transpose(back[:, at, :], scaled[:, m].rearrange("p g s -> p (g s)"), ident[:])
            nc.scalar.copy(right[:, tiles[0] : tiles[-1] + 1, P * unit : P * (unit + 1)], back[:])

        lefts = {}

        def scatter_through(unit):
            for m, lo, hi in SCATTERS:
                if (hi - 1) // P == unit:
                    nc.vector.tensor_tensor(
                        windows[m][:].indirect(place[:, lo // STRIPE : hi // STRIPE]),
                        lefts.get((m, lo), left[:, m, lo:hi]),
                        right[:, m, lo:hi],
                        MULT,
                    )
                    if hi == S:
                        nc.sync.dma_start(out=out[P * m : P * (m + 1), :], in_=windows[m][:])

        nc.gpsimd.tensor_tensor(right[:, 0, :P], first_gate(0, "b1")[:], weights[:], MULT)
        second_up = turned_up(1)
        nc.scalar.copy(left[:, 0, :P], first_up(0, "b3")[:])
        nc.vector.tensor_tensor(right[:, 1, :P], first_up(1, "b4")[:], weights[:], MULT)
        scaled = weigh(1, second_up)
        lefts[1, 0] = first_gate(1, "b5")[:]
        scatter_through(0)
        gate_unit(1)
        turn_back(1, scaled, (0,), "b6")
        turn_back(1, scaled, (1,), "b7")
        scatter_through(1)
        for unit in range(2, UNITS):
            scaled = weigh(unit, turned_up(unit))
            gate_unit(unit)
            if unit == 2:
                turn_back(unit, scaled, (0,), "b1")
                turn_back(unit, scaled, (1,), "b3")
            else:
                turn_back(unit, scaled, (0, 1), BACK_BANKS[unit])
            scatter_through(unit)
